import numpy as np
import ml_dtypes


def mxq(x, axis, fmt="e4m3"):
    dtype, down = {"e4m3": (ml_dtypes.float8_e4m3fn, 7), "e5m2": (ml_dtypes.float8_e5m2, 14)}[fmt]
    v = np.moveaxis(np.asarray(x, np.float32).astype(ml_dtypes.bfloat16).astype(np.float64), axis, -1)
    blocks = v.reshape(v.shape[:-1] + (-1, 32))
    amax = np.abs(blocks).max(-1, keepdims=True)
    byte = np.maximum(np.where(amax > 0, np.frexp(amax)[1] - 1 + 127, 0) - down, 1)
    scale = np.exp2(byte - 127.0)
    codes = (blocks / scale).astype(np.float32).astype(dtype).astype(np.float64)
    return np.moveaxis((codes * scale).reshape(v.shape), -1, axis)


WIDE = False


def mx_kscale(k):
    if not WIDE:
        return np.ones(k)
    levels = np.array([10, -10, 5, -5, 0])
    if k % 512:
        return np.exp2(np.random.permutation(np.resize(levels, k // 32))).repeat(32)
    a = np.empty((k // 512, 16))
    for p in range(k // 512):
        a[p, :8] = np.random.permutation(np.resize(levels, 8))
        for g in range(8):
            far = levels[np.abs(levels - a[p, g]) >= 10]
            a[p, g + 8] = far[np.random.randint(len(far))]
    return np.exp2(a.ravel()).repeat(32)


def f64(x):
    return np.asarray(x).astype(np.float64)


def striped(idx):
    return np.tile(idx.reshape(-1, 16).T, (8, 1)).astype(np.uint16)


def unstriped(offs):
    return offs[:16].T.reshape(-1).astype(np.int64)


def pack_weight(w):
    k, n = w.shape
    w = f64(np.asarray(w, np.float32).astype(ml_dtypes.bfloat16)).reshape(k // 32, 32, n)
    amax = np.abs(w).max(1)
    byte = np.clip(np.where(amax > 0, np.frexp(amax)[1] - 1 + 127 - 7, 1), 1, 254)
    scaled = (w * np.exp2(127.0 - byte)[:, None, :]).reshape(k, n).astype(np.float32)
    words = np.ascontiguousarray(scaled.reshape(k // 512, 128, 4, n).transpose(0, 1, 3, 2)).astype(ml_dtypes.float8_e4m3fn).view(np.uint8)
    return words, np.ascontiguousarray(byte.astype(np.uint8).reshape(k // 512, 16, n))


def unpack_weight(words, scales):
    g, p, n, _ = words.shape
    vals = np.ascontiguousarray(words).view(ml_dtypes.float8_e4m3fn).astype(np.float64) * np.repeat(np.exp2(scales.astype(np.float64) - 127.0), 8, axis=1)[..., None]
    return vals.transpose(0, 1, 3, 2).reshape(g * 512, n)


def relu(v):
    return np.maximum(v, 0.0)


K, T, S, V, H, W, G = 512, 1024, 512, 512, 512, 1024, 1024


def setup_inputs():
    n = np.random.standard_normal
    s = mx_kscale(K)[:, None]
    u = mx_kscale(H)
    packed_xT = pack_weight(n((K, T)) * s)
    packed_eT = pack_weight(n((K, W)) / np.sqrt(2 * K) / s)
    packed_vT = pack_weight(n((H, G)) / np.sqrt(2 * H) / u[:, None])
    return {
        "x_words": packed_xT[0],
        "x_scales": packed_xT[1],
        "e_words": packed_eT[0],
        "e_scales": packed_eT[1],
        "v_words": packed_vT[0],
        "v_scales": packed_vT[1],
        "gT": (n((K, S)) * s).astype(np.float32),
        "w1": (n((K, H)) / np.sqrt(K) / s * u).astype(np.float32),
        "offs": striped(np.random.permutation(T)[:S]),
        "cand": striped(np.random.permutation(W)[:V]),
    }


def reference(x_words, x_scales, e_words, e_scales, v_words, v_scales, gT, w1, offs, cand):
    xq = unpack_weight(x_words, x_scales)[:, unstriped(offs)]
    e_cand = unpack_weight(e_words, e_scales)[:, unstriped(cand)]
    gTq = mxq(f64(gT), 0, "e4m3")
    h = relu(mxq(f64(w1), 0, "e4m3").T @ gTq)
    v_cand = unpack_weight(v_words, v_scales)[:, unstriped(cand)]
    y = xq.T @ e_cand + mxq(h, 0, "e4m3").T @ v_cand
    e = np.exp(y - y.max(axis=1, keepdims=True))
    return e / e.sum(axis=1, keepdims=True)

@@ -1,0 +1,203 @@
+from contextlib import ExitStack
+
+import concourse.mybir as mybir
+
+K, T, S, V, H = 512, 1024, 512, 512, 512
+FLOPS = 2 * K * H * S + 2 * K * S * V + 2 * H * S * V
+
+F32 = mybir.dt.float32
+BF16 = mybir.dt.bfloat16
+I32 = mybir.dt.int32
+U32 = mybir.dt.uint32
+U16 = mybir.dt.uint16
+U8 = mybir.dt.uint8
+FP8X4 = mybir.dt.float8_e4m3fn_x4
+ACT = mybir.ActivationFunctionType
+ALU = mybir.AluOpType
+AX = mybir.AxisListType
+
+P = 128
+PACK = 4
+CH = 128
+NCH = S // CH
+
+
+def tile_picked_zwd_soft_p_kernel(tc, x_words, x_scales, e_words, e_scales, v_words, v_scales, gT, w1, offs, cand, out):
+    nc = tc.nc
+    with ExitStack() as ctx:
+        sb = ctx.enter_context(tc.tile_pool(name="sb", bufs=1))
+        ps = ctx.enter_context(tc.psum_pool(name="ps", bufs=1))
+
+        def tile(name, shape, dt):
+            return sb.tile(shape, dt, name=name, align_bytes=64)
+
+        cand_t = tile("cand_t", [P, V // 16], U16)
+        offs_t = tile("offs_t", [P, S // 16], U16)
+        warm = tile("warm", [P, 1], F32)
+        warm2 = tile("warm2", [P, 1], F32)
+        nc.vector.memset(warm[:], 0.0)
+        nc.scalar.activation(warm2[:], warm[:], ACT.Exp)
+
+        def load_scale_rows(t, src, q, queue, spread):
+            words = t[:].bitcast(I32)
+            quad = src[0].bitcast(I32)[4 * q : 4 * q + 4, :]
+            if spread:
+                queue.dma_start(out=words[32 * q : 32 * q + 32, :], in_=quad.unsqueeze(0).to_broadcast([8, 4, T // 4]))
+            else:
+                queue.dma_start(out=words[32 * q : 32 * q + 4, :], in_=quad)
+
+        es_w = tile("es_w", [P, T], U8)
+        vs_w = tile("vs_w", [P, T], U8)
+        xs_w = tile("xs_w", [P, T], U8)
+        ew = tile("ew", [P, T], I32)
+        vw = tile("vw", [P, T], I32)
+        xw = tile("xw", [P, T], I32)
+        nc.vector.memset(vs_w[:].bitcast(I32), 0)
+        nc.vector.memset(xs_w[:].bitcast(I32), 0)
+        w_src = w1.rearrange("(p j) c -> p j c", j=PACK)
+        g_src = gT.rearrange("(p j) c -> p j c", j=PACK)
+        w_raw = [tile(f"w_raw{u}", [P, PACK, 256], F32) for u in range(2)]
+        g_raw = [tile(f"g_raw{u}", [P, PACK, 256], F32) for u in range(2)]
+        nc.sync.dma_start(cand_t[:], cand)
+        load_scale_rows(es_w, e_scales, 2, nc.scalar, True)
+        load_scale_rows(es_w, e_scales, 0, nc.sync, True)
+        load_scale_rows(es_w, e_scales, 3, nc.scalar, True)
+        load_scale_rows(es_w, e_scales, 1, nc.sync, True)
+        nc.sync.dma_start(out=ew[:], in_=e_words[0].rearrange("p n t -> p (n t)").bitcast(I32))
+        nc.sync.dma_start(out=w_raw[0][:], in_=w_src[:, :, 256 * 0 : 256 * 1])
+        load_scale_rows(vs_w, v_scales, 0, nc.sync, False)
+        load_scale_rows(vs_w, v_scales, 1, nc.sync, False)
+        load_scale_rows(vs_w, v_scales, 2, nc.sync, False)
+        load_scale_rows(vs_w, v_scales, 3, nc.sync, False)
+        nc.sync.dma_start(out=w_raw[1][:], in_=w_src[:, :, 256 * 1 : 256 * 2])
+        nc.sync.dma_start(out=g_raw[0][:], in_=g_src[:, :, 256 * 0 : 256 * 1])
+        nc.sync.dma_start(offs_t[:], offs)
+        load_scale_rows(xs_w, x_scales, 0, nc.sync, False)
+        load_scale_rows(xs_w, x_scales, 1, nc.sync, False)
+        load_scale_rows(xs_w, x_scales, 2, nc.sync, False)
+        load_scale_rows(xs_w, x_scales, 3, nc.sync, False)
+        nc.sync.dma_start(out=g_raw[1][:], in_=g_src[:, :, 256 * 1 : 256 * 2])
+        nc.sync.dma_start(out=vw[:], in_=v_words[0].rearrange("p n t -> p (n t)").bitcast(I32))
+        nc.sync.dma_start(out=xw[:], in_=x_words[0].rearrange("p n t -> p (n t)").bitcast(I32))
+
+        es = tile("es", [P, V], U8)
+        vs = tile("vs", [P, V], U8)
+        xs = tile("xs", [P, S], U8)
+        eq = tile("eq", [P, V], U32)
+        vq = tile("vq", [P, V], U32)
+        w_bf = tile("w_bf", [P, H * PACK], BF16)
+        w_view = w_bf[:].rearrange("p (t m j) -> p m j t", t=PACK, j=PACK)
+        wq = tile("wq", [P, H], U32)
+        wsc = tile("wsc", [P, H], U8)
+        g_bf = [tile(f"g_bf{c}", [P, CH * PACK], BF16) for c in range(NCH)]
+        gq = [tile(f"gq{c}", [P, CH], U32) for c in range(NCH)]
+        gsc = [tile(f"gsc{c}", [P, CH], U8) for c in range(NCH)]
+        h_ps = [ps.tile([P, PACK, CH], F32, name=f"h_ps{c}") for c in range(NCH)]
+        y_ps = [ps.tile([P, V], F32, name=f"y_ps{c}") for c in range(NCH)]
+        h_bf = [tile(f"h_bf{c}", [P, CH * PACK], BF16) for c in range(NCH)]
+        hq = [tile(f"hq{c}", [P, CH], U32) for c in range(NCH)]
+        hsc = [tile(f"hsc{c}", [P, CH], U8) for c in range(NCH)]
+        xq = [tile(f"xq{c}", [P, CH], U32) for c in range(NCH)]
+        neg_max = [tile(f"neg_max{c}", [P, 1], F32) for c in range(NCH)]
+        total = [tile(f"total{c}", [P, 1], F32) for c in range(NCH)]
+        inv = [tile(f"inv{c}", [P, 1], F32) for c in range(NCH)]
+        ex = [tile(f"ex{c}", [P, V], F32) for c in range(NCH)]
+        res = [tile(f"res{c}", [P, V], F32) for c in range(NCH)]
+
+        def copy(eng, dst, src):
+            if eng == "v":
+                nc.vector.tensor_copy(dst, src)
+            elif eng == "g":
+                nc.gpsimd.tensor_copy(dst, src)
+            else:
+                nc.scalar.copy(dst, src)
+
+        def gather(dst, window, offsets):
+            nc.vector.tensor_copy(dst, window.indirect(offsets))
+
+        def cast_w(u, eng, a=0, b=64):
+            copy(eng, w_view[:, 64 * u + a : 64 * u + b], w_raw[u][:].rearrange("p j (m t) -> p m j t", t=PACK)[:, a:b])
+
+        def quant_w():
+            nc.vector.quantize_mx(out=wq[:].bitcast(FP8X4), scales=wsc[:], in_=w_bf[:])
+
+        def cast_g(c, eng):
+            raw = g_raw[c // 2][:, :, CH * (c % 2) : CH * (c % 2 + 1)]
+            copy(eng, g_bf[c][:].rearrange("p (n i j) -> p n j i", i=4, j=PACK), raw.rearrange("p j (n i) -> p n j i", i=4))
+
+        def quant_g(c):
+            nc.vector.quantize_mx(out=gq[c][:].bitcast(FP8X4), scales=gsc[c][:], in_=g_bf[c][:])
+
+        def mm_h(c):
+            for j in range(PACK):
+                cols = slice(P * j, P * (j + 1))
+                nc.tensor.matmul_mx(out=h_ps[c][:, j, :], lhsT=wq[:, cols].bitcast(FP8X4), lhsT_scale=wsc[:, cols],
+                                    rhs=gq[c][:].bitcast(FP8X4), rhs_scale=gsc[c][:], start=True, stop=True)
+
+        def relu(c, eng="s"):
+            dst = h_bf[c][:].rearrange("p (n j) -> p n j", j=PACK)
+            src = h_ps[c][:].rearrange("p j n -> p n j")
+            if eng == "s":
+                nc.scalar.activation(dst, src, ACT.Relu)
+            else:
+                nc.vector.tensor_scalar(dst, src, 0.0, None, ALU.max)
+
+        def quant_h(c):
+            nc.vector.quantize_mx(out=hq[c][:].bitcast(FP8X4), scales=hsc[c][:], in_=h_bf[c][:])
+
+        def mm_deep(c, first):
+            nc.tensor.matmul_mx(out=y_ps[c][:], lhsT=hq[c][:].bitcast(FP8X4), lhsT_scale=hsc[c][:],
+                                rhs=vq[:].bitcast(FP8X4), rhs_scale=vs[:], start=first, stop=not first)
+
+        def gather_x(c):
+            gather(xq[c][:], xw[:].bitcast(U32), offs_t[:, 8 * c : 8 * (c + 1)])
+
+        def mm_wide(c, first):
+            nc.tensor.matmul_mx(out=y_ps[c][:], lhsT=xq[c][:].bitcast(FP8X4), lhsT_scale=xs[:, CH * c : CH * (c + 1)],
+                                rhs=eq[:].bitcast(FP8X4), rhs_scale=es[:], start=first, stop=not first)
+
+        def row_max(c):
+            nc.vector.tensor_reduce(neg_max[c][:], y_ps[c][:], AX.X, ALU.max, negate=True)
+
+        def exp(c):
+            nc.scalar.activation(ex[c][:], y_ps[c][:], ACT.Exp, bias=neg_max[c][:], accum_out=total[c][:])
+
+        def recip(c):
+            nc.vector.reciprocal(inv[c][:], total[c][:])
+
+        def norm(c, eng, a=0, b=V):
+            if eng == "g":
+                nc.gpsimd.tensor_scalar(res[c][:, a:b], ex[c][:, a:b], inv[c][:], 0.0, ALU.mult, ALU.add)
+            elif eng == "v":
+                nc.vector.tensor_scalar(res[c][:, a:b], ex[c][:, a:b], inv[c][:], None, ALU.mult)
+            else:
+                nc.scalar.activation(res[c][:, a:b], ex[c][:, a:b], ACT.Copy, scale=inv[c][:])
+
+        def store(c, queue, a=0, b=V):
+            queue.dma_start(out=out[CH * c : CH * (c + 1), a:b], in_=res[c][:, a:b])
+
+        gather(es[:], es_w[:], cand_t[:])
+        gather(eq[:], ew[:].bitcast(U32), cand_t[:])
+        gather(vs[:], vs_w[:], cand_t[:])
+        cast_w(0, "s")
+        cast_w(1, "v")
+        quant_w()
+        gather(xs[:], xs_w[:], offs_t[:])
+        for c in range(NCH):
+            cast_g(c, "s")
+            quant_g(c)
+            mm_h(c)
+        gather(vq[:], vw[:].bitcast(U32), cand_t[:])
+        for c in range(NCH):
+            relu(c)
+            quant_h(c)
+            mm_deep(c, True)
+        for c in range(NCH):
+            gather_x(c)
+            mm_wide(c, False)
+        for c in range(NCH):
+            row_max(c)
+            exp(c)
+            recip(c)
+            norm(c, "g" if c < 3 else "v")
+            store(c, nc.sync)

@@ -35,16 +35,9 @@ def tile_picked_zwd_soft_p_kernel(tc, x_words, x_scales, e_words, e_scales, v_wo
         offs_t = tile("offs_t", [P, S // 16], U16)
         warm = tile("warm", [P, 1], F32)
         warm2 = tile("warm2", [P, 1], F32)
-        nc.vector.memset(warm[:], 0.0)
-        nc.scalar.activation(warm2[:], warm[:], ACT.Exp)
 
-        def load_scale_rows(t, src, q, queue, spread):
-            words = t[:].bitcast(I32)
-            quad = src[0].bitcast(I32)[4 * q : 4 * q + 4, :]
-            if spread:
-                queue.dma_start(out=words[32 * q : 32 * q + 32, :], in_=quad.unsqueeze(0).to_broadcast([8, 4, T // 4]))
-            else:
-                queue.dma_start(out=words[32 * q : 32 * q + 4, :], in_=quad)
+        def load_scale_rows(t, src, r, queue):
+            queue.dma_start(out=t[:].bitcast(I32)[r:P:32, :], in_=src[0].bitcast(I32)[r:16:4, :])
 
         es_w = tile("es_w", [P, T], U8)
         vs_w = tile("vs_w", [P, T], U8)
@@ -52,33 +45,12 @@ def tile_picked_zwd_soft_p_kernel(tc, x_words, x_scales, e_words, e_scales, v_wo
         ew = tile("ew", [P, T], I32)
         vw = tile("vw", [P, T], I32)
         xw = tile("xw", [P, T], I32)
-        nc.vector.memset(vs_w[:].bitcast(I32), 0)
-        nc.vector.memset(xs_w[:].bitcast(I32), 0)
+
         w_src = w1.rearrange("(p j) c -> p j c", j=PACK)
         g_src = gT.rearrange("(p j) c -> p j c", j=PACK)
         w_raw = [tile(f"w_raw{u}", [P, PACK, 256], F32) for u in range(2)]
-        g_raw = [tile(f"g_raw{u}", [P, PACK, 256], F32) for u in range(2)]
-        nc.sync.dma_start(cand_t[:], cand)
-        load_scale_rows(es_w, e_scales, 2, nc.scalar, True)
-        load_scale_rows(es_w, e_scales, 0, nc.sync, True)
-        load_scale_rows(es_w, e_scales, 3, nc.scalar, True)
-        load_scale_rows(es_w, e_scales, 1, nc.sync, True)
-        nc.sync.dma_start(out=ew[:], in_=e_words[0].rearrange("p n t -> p (n t)").bitcast(I32))
-        nc.sync.dma_start(out=w_raw[0][:], in_=w_src[:, :, 256 * 0 : 256 * 1])
-        load_scale_rows(vs_w, v_scales, 0, nc.sync, False)
-        load_scale_rows(vs_w, v_scales, 1, nc.sync, False)
-        load_scale_rows(vs_w, v_scales, 2, nc.sync, False)
-        load_scale_rows(vs_w, v_scales, 3, nc.sync, False)
-        nc.sync.dma_start(out=w_raw[1][:], in_=w_src[:, :, 256 * 1 : 256 * 2])
-        nc.sync.dma_start(out=g_raw[0][:], in_=g_src[:, :, 256 * 0 : 256 * 1])
-        nc.sync.dma_start(offs_t[:], offs)
-        load_scale_rows(xs_w, x_scales, 0, nc.sync, False)
-        load_scale_rows(xs_w, x_scales, 1, nc.sync, False)
-        load_scale_rows(xs_w, x_scales, 2, nc.sync, False)
-        load_scale_rows(xs_w, x_scales, 3, nc.sync, False)
-        nc.sync.dma_start(out=g_raw[1][:], in_=g_src[:, :, 256 * 1 : 256 * 2])
-        nc.sync.dma_start(out=vw[:], in_=v_words[0].rearrange("p n t -> p (n t)").bitcast(I32))
-        nc.sync.dma_start(out=xw[:], in_=x_words[0].rearrange("p n t -> p (n t)").bitcast(I32))
+        g_raw = [sb.tile([P, PACK, 256], F32, name=f"g_raw{u}", tag=f"g_raw{u}", align_bytes=64) for u in range(2)]
+
 
         es = tile("es", [P, V], U8)
         vs = tile("vs", [P, V], U8)
@@ -94,7 +66,7 @@ def tile_picked_zwd_soft_p_kernel(tc, x_words, x_scales, e_words, e_scales, v_wo
         gsc = [tile(f"gsc{c}", [P, CH], U8) for c in range(NCH)]
         h_ps = [ps.tile([P, PACK, CH], F32, name=f"h_ps{c}") for c in range(NCH)]
         y_ps = [ps.tile([P, V], F32, name=f"y_ps{c}") for c in range(NCH)]
-        h_bf = [tile(f"h_bf{c}", [P, CH * PACK], BF16) for c in range(NCH)]
+        h_bf = {}
         hq = [tile(f"hq{c}", [P, CH], U32) for c in range(NCH)]
         hsc = [tile(f"hsc{c}", [P, CH], U8) for c in range(NCH)]
         xq = [tile(f"xq{c}", [P, CH], U32) for c in range(NCH)]
@@ -135,7 +107,13 @@ def tile_picked_zwd_soft_p_kernel(tc, x_words, x_scales, e_words, e_scales, v_wo
                                     rhs=gq[c][:].bitcast(FP8X4), rhs_scale=gsc[c][:], start=True, stop=True)
 
         def relu(c, eng="s"):
-            dst = h_bf[c][:].rearrange("p (n j) -> p n j", j=PACK)
+            if c == 0:
+                pair = sb.tile([P, 2 * CH * PACK], BF16, name="h_pair", tag="g_raw1", align_bytes=64)
+                h_bf[0] = pair[:, : CH * PACK]
+                h_bf[1] = pair[:, CH * PACK :]
+            elif c > 1:
+                h_bf[c] = tile(f"h_bf{c}", [P, CH * PACK], BF16)[:]
+            dst = h_bf[c].rearrange("p (n j) -> p n j", j=PACK)
             src = h_ps[c][:].rearrange("p j n -> p n j")
             if eng == "s":
                 nc.scalar.activation(dst, src, ACT.Relu)
@@ -143,7 +121,7 @@ def tile_picked_zwd_soft_p_kernel(tc, x_words, x_scales, e_words, e_scales, v_wo
                 nc.vector.tensor_scalar(dst, src, 0.0, None, ALU.max)
 
         def quant_h(c):
-            nc.vector.quantize_mx(out=hq[c][:].bitcast(FP8X4), scales=hsc[c][:], in_=h_bf[c][:])
+            nc.vector.quantize_mx(out=hq[c][:].bitcast(FP8X4), scales=hsc[c][:], in_=h_bf[c])
 
         def mm_deep(c, first):
             nc.tensor.matmul_mx(out=y_ps[c][:], lhsT=hq[c][:].bitcast(FP8X4), lhsT_scale=hsc[c][:],
@@ -176,28 +154,90 @@ def tile_picked_zwd_soft_p_kernel(tc, x_words, x_scales, e_words, e_scales, v_wo
         def store(c, queue, a=0, b=V):
             queue.dma_start(out=out[CH * c : CH * (c + 1), a:b], in_=res[c][:, a:b])
 
-        gather(es[:], es_w[:], cand_t[:])
+        nc.vector.memset(vs_w[:].bitcast(I32), 0)
+        nc.vector.memset(warm[:], 0.0)
+        nc.scalar.activation(warm2[:], warm[:], ACT.Exp)
+        nc.vector.memset(es_w[:].bitcast(I32), 0)
+        nc.vector.memset(xs_w[:].bitcast(I32), 0)
+        nc.sync.dma_start(out=ew[:], in_=e_words[0].rearrange("p n t -> p (n t)").bitcast(I32))
+        nc.sync.dma_start(cand_t[:], cand)
+        load_scale_rows(vs_w, v_scales, 0, nc.sync)
+        load_scale_rows(vs_w, v_scales, 1, nc.sync)
+        load_scale_rows(vs_w, v_scales, 2, nc.sync)
+        load_scale_rows(vs_w, v_scales, 3, nc.sync)
+        nc.sync.dma_start(out=w_raw[0][:], in_=w_src[:, :, 256 * 0 : 256 * 1])
+        nc.sync.dma_start(out=w_raw[1][:], in_=w_src[:, :, 256 * 1 : 256 * 2])
+        load_scale_rows(es_w, e_scales, 0, nc.sync)
+        load_scale_rows(es_w, e_scales, 1, nc.sync)
+        load_scale_rows(es_w, e_scales, 2, nc.sync)
+        load_scale_rows(es_w, e_scales, 3, nc.sync)
+        nc.sync.dma_start(offs_t[:], offs)
+        nc.sync.dma_start(out=g_raw[0][:], in_=g_src[:, :, 256 * 0 : 256 * 1])
+        load_scale_rows(xs_w, x_scales, 0, nc.sync)
+        load_scale_rows(xs_w, x_scales, 1, nc.sync)
+        load_scale_rows(xs_w, x_scales, 2, nc.sync)
+        nc.sync.dma_start(out=g_raw[1][:], in_=g_src[:, :, 256 * 1 : 256 * 2])
+        load_scale_rows(xs_w, x_scales, 3, nc.sync)
+        nc.sync.dma_start(out=vw[:], in_=v_words[0].rearrange("p n t -> p (n t)").bitcast(I32))
+        nc.sync.dma_start(out=xw[:], in_=x_words[0].rearrange("p n t -> p (n t)").bitcast(I32))
         gather(eq[:], ew[:].bitcast(U32), cand_t[:])
         gather(vs[:], vs_w[:], cand_t[:])
         cast_w(0, "s")
-        cast_w(1, "v")
+        cast_w(1, "v", 0, 32)
+        cast_w(1, "s", 32, 64)
         quant_w()
+        gather(es[:], es_w[:], cand_t[:])
+        cast_g(0, "s")
+        cast_g(1, "s")
+        cast_g(2, "s")
+        cast_g(3, "s")
+        quant_g(0)
+        mm_h(0)
+        quant_g(1)
+        mm_h(1)
         gather(xs[:], xs_w[:], offs_t[:])
-        for c in range(NCH):
-            cast_g(c, "s")
-            quant_g(c)
-            mm_h(c)
+        quant_g(2)
+        mm_h(2)
+        quant_g(3)
+        mm_h(3)
         gather(vq[:], vw[:].bitcast(U32), cand_t[:])
-        for c in range(NCH):
-            relu(c)
-            quant_h(c)
-            mm_deep(c, True)
-        for c in range(NCH):
-            gather_x(c)
-            mm_wide(c, False)
-        for c in range(NCH):
-            row_max(c)
-            exp(c)
-            recip(c)
-            norm(c, "g" if c < 3 else "v")
-            store(c, nc.sync)
+        relu(0)
+        relu(1)
+        relu(2)
+        relu(3)
+        quant_h(0)
+        mm_deep(0, True)
+        quant_h(1)
+        mm_deep(1, True)
+        gather_x(0)
+        mm_wide(0, False)
+        gather_x(1)
+        mm_wide(1, False)
+        quant_h(2)
+        mm_deep(2, True)
+        gather_x(2)
+        mm_wide(2, False)
+        quant_h(3)
+        mm_deep(3, True)
+        gather_x(3)
+        mm_wide(3, False)
+        row_max(0)
+        exp(0)
+        row_max(1)
+        exp(1)
+        row_max(2)
+        exp(2)
+        recip(0)
+        row_max(3)
+        exp(3)
+        norm(0, "v")
+        store(0, nc.sync)
+        recip(1)
+        norm(1, "v")
+        store(1, nc.sync)
+        recip(2)
+        norm(2, "v")
+        store(2, nc.sync)
+        recip(3)
+        norm(3, "v")
+        store(3, nc.sync)

@@ -154,10 +154,10 @@ def tile_picked_zwd_soft_p_kernel(tc, x_words, x_scales, e_words, e_scales, v_wo
         def store(c, queue, a=0, b=V):
             queue.dma_start(out=out[CH * c : CH * (c + 1), a:b], in_=res[c][:, a:b])
 
+        nc.gpsimd.memset(es_w[:].bitcast(I32), 0)
         nc.vector.memset(vs_w[:].bitcast(I32), 0)
         nc.vector.memset(warm[:], 0.0)
         nc.scalar.activation(warm2[:], warm[:], ACT.Exp)
-        nc.vector.memset(es_w[:].bitcast(I32), 0)
         nc.vector.memset(xs_w[:].bitcast(I32), 0)
         nc.sync.dma_start(out=ew[:], in_=e_words[0].rearrange("p n t -> p (n t)").bitcast(I32))
         nc.sync.dma_start(cand_t[:], cand)
@@ -166,36 +166,36 @@ def tile_picked_zwd_soft_p_kernel(tc, x_words, x_scales, e_words, e_scales, v_wo
         load_scale_rows(vs_w, v_scales, 2, nc.sync)
         load_scale_rows(vs_w, v_scales, 3, nc.sync)
         nc.sync.dma_start(out=w_raw[0][:], in_=w_src[:, :, 256 * 0 : 256 * 1])
-        nc.sync.dma_start(out=w_raw[1][:], in_=w_src[:, :, 256 * 1 : 256 * 2])
-        load_scale_rows(es_w, e_scales, 0, nc.sync)
-        load_scale_rows(es_w, e_scales, 1, nc.sync)
-        load_scale_rows(es_w, e_scales, 2, nc.sync)
-        load_scale_rows(es_w, e_scales, 3, nc.sync)
         nc.sync.dma_start(offs_t[:], offs)
-        nc.sync.dma_start(out=g_raw[0][:], in_=g_src[:, :, 256 * 0 : 256 * 1])
+        load_scale_rows(es_w, e_scales, 0, nc.gpsimd)
+        load_scale_rows(es_w, e_scales, 1, nc.gpsimd)
         load_scale_rows(xs_w, x_scales, 0, nc.sync)
         load_scale_rows(xs_w, x_scales, 1, nc.sync)
         load_scale_rows(xs_w, x_scales, 2, nc.sync)
-        nc.sync.dma_start(out=g_raw[1][:], in_=g_src[:, :, 256 * 1 : 256 * 2])
         load_scale_rows(xs_w, x_scales, 3, nc.sync)
+        load_scale_rows(es_w, e_scales, 2, nc.sync)
+        nc.sync.dma_start(out=w_raw[1][:], in_=w_src[:, :, 256 * 1 : 256 * 2])
+        load_scale_rows(es_w, e_scales, 3, nc.sync)
+        nc.sync.dma_start(out=g_raw[0][:], in_=g_src[:, :, 256 * 0 : 256 * 1])
+        nc.sync.dma_start(out=g_raw[1][:], in_=g_src[:, :, 256 * 1 : 256 * 2])
         nc.sync.dma_start(out=vw[:], in_=v_words[0].rearrange("p n t -> p (n t)").bitcast(I32))
         nc.sync.dma_start(out=xw[:], in_=x_words[0].rearrange("p n t -> p (n t)").bitcast(I32))
         gather(eq[:], ew[:].bitcast(U32), cand_t[:])
         gather(vs[:], vs_w[:], cand_t[:])
+        gather(xs[:], xs_w[:], offs_t[:])
         cast_w(0, "s")
-        cast_w(1, "v", 0, 32)
-        cast_w(1, "s", 32, 64)
+        cast_w(1, "v", 0, 38)
+        cast_w(1, "s", 38, 64)
         quant_w()
         gather(es[:], es_w[:], cand_t[:])
         cast_g(0, "s")
         cast_g(1, "s")
-        cast_g(2, "s")
         cast_g(3, "s")
         quant_g(0)
         mm_h(0)
         quant_g(1)
         mm_h(1)
-        gather(xs[:], xs_w[:], offs_t[:])
+        cast_g(2, "v")
         quant_g(2)
         mm_h(2)
         quant_g(3)

@@ -20,6 +20,7 @@ P = 128
 PACK = 4
 CH = 128
 NCH = S // CH
+HALF = 256
 
 
 def tile_picked_zwd_soft_p_kernel(tc, x_words, x_scales, e_words, e_scales, v_words, v_scales, gT, w1, offs, cand, out):
@@ -31,213 +32,168 @@ def tile_picked_zwd_soft_p_kernel(tc, x_words, x_scales, e_words, e_scales, v_wo
         def tile(name, shape, dt):
             return sb.tile(shape, dt, name=name, align_bytes=64)
 
+        def shared(name, shape, dt, tag):
+            return sb.tile(shape, dt, name=name, tag=tag, align_bytes=64)
+
         cand_t = tile("cand_t", [P, V // 16], U16)
         offs_t = tile("offs_t", [P, S // 16], U16)
-        warm = tile("warm", [P, 1], F32)
-        warm2 = tile("warm2", [P, 1], F32)
-
-        def load_scale_rows(t, src, r, queue):
-            queue.dma_start(out=t[:].bitcast(I32)[r:P:32, :], in_=src[0].bitcast(I32)[r:16:4, :])
-
-        es_w = tile("es_w", [P, T], U8)
-        vs_w = tile("vs_w", [P, T], U8)
-        xs_w = tile("xs_w", [P, T], U8)
-        ew = tile("ew", [P, T], I32)
-        vw = tile("vw", [P, T], I32)
-        xw = tile("xw", [P, T], I32)
-
+        es_w = shared("es_w", [P, T], U8, "es_w")
+        vs_w = shared("vs_w", [P, T], U8, "vs_w")
+        xs_w = shared("xs_w", [P, T], U8, "xs_w")
         w_src = w1.rearrange("(p j) c -> p j c", j=PACK)
         g_src = gT.rearrange("(p j) c -> p j c", j=PACK)
-        w_raw = [tile(f"w_raw{u}", [P, PACK, 256], F32) for u in range(2)]
-        g_raw = [sb.tile([P, PACK, 256], F32, name=f"g_raw{u}", tag=f"g_raw{u}", align_bytes=64) for u in range(2)]
-
-
-        es = tile("es", [P, V], U8)
-        vs = tile("vs", [P, V], U8)
-        xs = tile("xs", [P, S], U8)
-        eq = tile("eq", [P, V], U32)
-        vq = tile("vq", [P, V], U32)
-        w_bf = tile("w_bf", [P, H * PACK], BF16)
+        w_raw = tile("w_raw", [P, PACK, H], F32)
+        g_raw = [shared(f"g_raw{u}", [P, PACK, HALF], F32, f"g_raw{u}") for u in range(2)]
+        picked = tile("picked", [P, 2 * V + S], U8)
+        planes = tile("planes", [P, 2 * V + S], U8)
+        es, vs, xs = planes[:, :V], planes[:, V : 2 * V], planes[:, 2 * V :]
+        w_bf = shared("w_bf", [P, H * PACK], BF16, "w_bf")
         w_view = w_bf[:].rearrange("p (t m j) -> p m j t", t=PACK, j=PACK)
-        wq = tile("wq", [P, H], U32)
         wsc = tile("wsc", [P, H], U8)
-        g_bf = [tile(f"g_bf{c}", [P, CH * PACK], BF16) for c in range(NCH)]
-        gq = [tile(f"gq{c}", [P, CH], U32) for c in range(NCH)]
-        gsc = [tile(f"gsc{c}", [P, CH], U8) for c in range(NCH)]
+        gsc = tile("gsc", [P, S], U8)
+        hsc = tile("hsc", [P, S], U8)
         h_ps = [ps.tile([P, PACK, CH], F32, name=f"h_ps{c}") for c in range(NCH)]
         y_ps = [ps.tile([P, V], F32, name=f"y_ps{c}") for c in range(NCH)]
-        h_bf = {}
-        hq = [tile(f"hq{c}", [P, CH], U32) for c in range(NCH)]
-        hsc = [tile(f"hsc{c}", [P, CH], U8) for c in range(NCH)]
-        xq = [tile(f"xq{c}", [P, CH], U32) for c in range(NCH)]
-        neg_max = [tile(f"neg_max{c}", [P, 1], F32) for c in range(NCH)]
-        total = [tile(f"total{c}", [P, 1], F32) for c in range(NCH)]
+        h_all = tile("h_all", [P, S * PACK], BF16)
+        g_bf, gq, hq, xq = {}, {}, {}, {}
+        neg_max = [shared(f"neg_max{c}", [P, 1], F32, f"neg_max{c}") for c in range(NCH)]
+        total = [shared(f"total{c}", [P, 1], F32, f"total{c}") for c in range(NCH)]
         inv = [tile(f"inv{c}", [P, 1], F32) for c in range(NCH)]
         ex = [tile(f"ex{c}", [P, V], F32) for c in range(NCH)]
         res = [tile(f"res{c}", [P, V], F32) for c in range(NCH)]
 
+        def cols(c):
+            return slice(CH * c, CH * (c + 1))
+
+        def load_scales(t, src):
+            nc.sync.dma_start(out=t[:].bitcast(I32)[0:P:8, :], in_=src[0].bitcast(I32))
+
+        def load_words(t, src):
+            nc.sync.dma_start(out=t[:], in_=src[0].rearrange("p n t -> p (n t)").bitcast(I32))
+
+        def load_half(raw, src, u):
+            nc.sync.dma_start(out=raw[u][:], in_=src[:, :, HALF * u : HALF * (u + 1)])
+
+        def lay_planes():
+            for r in range(4):
+                nc.sync.dma_start(out=planes[:].bitcast(I32)[r:P:32, :], in_=picked[:].bitcast(I32)[8 * r : P : 32, :])
+
         def copy(eng, dst, src):
             if eng == "v":
                 nc.vector.tensor_copy(dst, src)
-            elif eng == "g":
-                nc.gpsimd.tensor_copy(dst, src)
             else:
                 nc.scalar.copy(dst, src)
 
         def gather(dst, window, offsets):
             nc.vector.tensor_copy(dst, window.indirect(offsets))
 
-        def cast_w(u, eng, a=0, b=64):
-            copy(eng, w_view[:, 64 * u + a : 64 * u + b], w_raw[u][:].rearrange("p j (m t) -> p m j t", t=PACK)[:, a:b])
+        def quant(codes, scales, src):
+            nc.vector.quantize_mx(out=codes.bitcast(FP8X4), scales=scales, in_=src)
 
-        def quant_w():
-            nc.vector.quantize_mx(out=wq[:].bitcast(FP8X4), scales=wsc[:], in_=w_bf[:])
+        def mm(dst, lhs, lhs_scale, rhs, rhs_scale, start, stop):
+            nc.tensor.matmul_mx(out=dst, lhsT=lhs.bitcast(FP8X4), lhsT_scale=lhs_scale,
+                                rhs=rhs.bitcast(FP8X4), rhs_scale=rhs_scale, start=start, stop=stop)
 
-        def cast_g(c, eng):
-            raw = g_raw[c // 2][:, :, CH * (c % 2) : CH * (c % 2 + 1)]
-            copy(eng, g_bf[c][:].rearrange("p (n i j) -> p n j i", i=4, j=PACK), raw.rearrange("p j (n i) -> p n j i", i=4))
+        def cast_w():
+            nc.scalar.copy(w_view, w_raw[:].rearrange("p j (m t) -> p m j t", t=PACK))
 
-        def quant_g(c):
-            nc.vector.quantize_mx(out=gq[c][:].bitcast(FP8X4), scales=gsc[c][:], in_=g_bf[c][:])
+        def cast_g(c, eng, tag):
+            g_bf[c] = shared(f"g_bf{c}", [P, CH * PACK], BF16, tag)[:]
+            raw = g_raw[c // 2][:, :, cols(c % 2)]
+            copy(eng, g_bf[c].rearrange("p (n i j) -> p n j i", i=4, j=PACK), raw.rearrange("p j (n i) -> p n j i", i=4))
 
-        def mm_h(c):
+        def layer1(c, tag):
+            gq[c] = shared(f"gq{c}", [P, CH], U32, tag)[:]
+            quant(gq[c], gsc[:, cols(c)], g_bf[c])
             for j in range(PACK):
-                cols = slice(P * j, P * (j + 1))
-                nc.tensor.matmul_mx(out=h_ps[c][:, j, :], lhsT=wq[:, cols].bitcast(FP8X4), lhsT_scale=wsc[:, cols],
-                                    rhs=gq[c][:].bitcast(FP8X4), rhs_scale=gsc[c][:], start=True, stop=True)
+                mm(h_ps[c][:, j, :], wq[:, cols(j)], wsc[:, cols(j)], gq[c], gsc[:, cols(c)], True, True)
 
-        def relu(c, eng="s"):
-            if c == 0:
-                pair = sb.tile([P, 2 * CH * PACK], BF16, name="h_pair", tag="g_raw1", align_bytes=64)
-                h_bf[0] = pair[:, : CH * PACK]
-                h_bf[1] = pair[:, CH * PACK :]
-            elif c > 1:
-                h_bf[c] = tile(f"h_bf{c}", [P, CH * PACK], BF16)[:]
-            dst = h_bf[c].rearrange("p (n j) -> p n j", j=PACK)
-            src = h_ps[c][:].rearrange("p j n -> p n j")
-            if eng == "s":
-                nc.scalar.activation(dst, src, ACT.Relu)
-            else:
-                nc.vector.tensor_scalar(dst, src, 0.0, None, ALU.max)
+        def relu(c):
+            nc.scalar.activation(h_all[:, CH * PACK * c : CH * PACK * (c + 1)].rearrange("p (n j) -> p n j", j=PACK), h_ps[c][:].rearrange("p j n -> p n j"), ACT.Relu)
 
-        def quant_h(c):
-            nc.vector.quantize_mx(out=hq[c][:].bitcast(FP8X4), scales=hsc[c][:], in_=h_bf[c])
+        def deep(first, n):
+            span = slice(CH * first, CH * (first + n))
+            quant(hq_all[:, span], hsc[:, span], h_all[:, CH * PACK * first : CH * PACK * (first + n)])
+            for c in range(first, first + n):
+                mm(y_ps[c][:], hq_all[:, cols(c)], hsc[:, cols(c)], vq[:], vs, False, True)
 
-        def mm_deep(c, first):
-            nc.tensor.matmul_mx(out=y_ps[c][:], lhsT=hq[c][:].bitcast(FP8X4), lhsT_scale=hsc[c][:],
-                                rhs=vq[:].bitcast(FP8X4), rhs_scale=vs[:], start=first, stop=not first)
+        def wide(c, first):
+            gather(xq[c], xw[:].bitcast(U32), offs_t[:, 8 * c : 8 * (c + 1)])
+            mm(y_ps[c][:], xq[c], xs[:, cols(c)], eq[:], es, first, not first)
 
-        def gather_x(c):
-            gather(xq[c][:], xw[:].bitcast(U32), offs_t[:, 8 * c : 8 * (c + 1)])
-
-        def mm_wide(c, first):
-            nc.tensor.matmul_mx(out=y_ps[c][:], lhsT=xq[c][:].bitcast(FP8X4), lhsT_scale=xs[:, CH * c : CH * (c + 1)],
-                                rhs=eq[:].bitcast(FP8X4), rhs_scale=es[:], start=first, stop=not first)
-
-        def row_max(c):
+        def max_exp(c):
             nc.vector.tensor_reduce(neg_max[c][:], y_ps[c][:], AX.X, ALU.max, negate=True)
-
-        def exp(c):
             nc.scalar.activation(ex[c][:], y_ps[c][:], ACT.Exp, bias=neg_max[c][:], accum_out=total[c][:])
 
         def recip(c):
             nc.vector.reciprocal(inv[c][:], total[c][:])
 
-        def norm(c, eng, a=0, b=V):
-            if eng == "g":
-                nc.gpsimd.tensor_scalar(res[c][:, a:b], ex[c][:, a:b], inv[c][:], 0.0, ALU.mult, ALU.add)
-            elif eng == "v":
-                nc.vector.tensor_scalar(res[c][:, a:b], ex[c][:, a:b], inv[c][:], None, ALU.mult)
+        def finish(c, eng):
+            if eng == "s":
+                nc.scalar.activation(res[c][:], ex[c][:], ACT.Copy, scale=inv[c][:])
+            elif eng == "g":
+                nc.gpsimd.tensor_scalar(res[c][:], ex[c][:], inv[c][:], 0.0, ALU.mult, ALU.add)
             else:
-                nc.scalar.activation(res[c][:, a:b], ex[c][:, a:b], ACT.Copy, scale=inv[c][:])
+                nc.vector.tensor_scalar(res[c][:], ex[c][:], inv[c][:], None, ALU.mult)
+            nc.sync.dma_start(out=out[cols(c), :], in_=res[c][:])
 
-        def store(c, queue, a=0, b=V):
-            queue.dma_start(out=out[CH * c : CH * (c + 1), a:b], in_=res[c][:, a:b])
-
-        nc.gpsimd.memset(es_w[:].bitcast(I32), 0)
-        nc.vector.memset(vs_w[:].bitcast(I32), 0)
+        warm = tile("warm", [P, 1], F32)
+        warm2 = tile("warm2", [P, 1], F32)
+        nc.vector.memset(es_w[:].bitcast(I32), 0)
+        nc.gpsimd.memset(vs_w[:].bitcast(I32), 0)
+        nc.vector.memset(xs_w[:].bitcast(I32), 0)
         nc.vector.memset(warm[:], 0.0)
         nc.scalar.activation(warm2[:], warm[:], ACT.Exp)
-        nc.vector.memset(xs_w[:].bitcast(I32), 0)
-        nc.sync.dma_start(out=ew[:], in_=e_words[0].rearrange("p n t -> p (n t)").bitcast(I32))
+        nc.gpsimd.memset(planes[:].bitcast(I32), 0)
+        vw = shared("vw", [P, T], I32, "vw")
+        ew = shared("ew", [P, T], I32, "ew")
+        xw = tile("xw", [P, T], I32)
         nc.sync.dma_start(cand_t[:], cand)
-        load_scale_rows(vs_w, v_scales, 0, nc.sync)
-        load_scale_rows(vs_w, v_scales, 1, nc.sync)
-        load_scale_rows(vs_w, v_scales, 2, nc.sync)
-        load_scale_rows(vs_w, v_scales, 3, nc.sync)
-        nc.sync.dma_start(out=w_raw[0][:], in_=w_src[:, :, 256 * 0 : 256 * 1])
+        nc.sync.dma_start(out=w_raw[:, :1, :], in_=w_src[:, :1, :])
+        load_scales(es_w, e_scales)
+        load_scales(vs_w, v_scales)
         nc.sync.dma_start(offs_t[:], offs)
-        load_scale_rows(es_w, e_scales, 0, nc.gpsimd)
-        load_scale_rows(es_w, e_scales, 1, nc.gpsimd)
-        load_scale_rows(xs_w, x_scales, 0, nc.sync)
-        load_scale_rows(xs_w, x_scales, 1, nc.sync)
-        load_scale_rows(xs_w, x_scales, 2, nc.sync)
-        load_scale_rows(xs_w, x_scales, 3, nc.sync)
-        load_scale_rows(es_w, e_scales, 2, nc.sync)
-        nc.sync.dma_start(out=w_raw[1][:], in_=w_src[:, :, 256 * 1 : 256 * 2])
-        load_scale_rows(es_w, e_scales, 3, nc.sync)
-        nc.sync.dma_start(out=g_raw[0][:], in_=g_src[:, :, 256 * 0 : 256 * 1])
-        nc.sync.dma_start(out=g_raw[1][:], in_=g_src[:, :, 256 * 1 : 256 * 2])
-        nc.sync.dma_start(out=vw[:], in_=v_words[0].rearrange("p n t -> p (n t)").bitcast(I32))
-        nc.sync.dma_start(out=xw[:], in_=x_words[0].rearrange("p n t -> p (n t)").bitcast(I32))
-        gather(eq[:], ew[:].bitcast(U32), cand_t[:])
-        gather(vs[:], vs_w[:], cand_t[:])
-        gather(xs[:], xs_w[:], offs_t[:])
-        cast_w(0, "s")
-        cast_w(1, "v", 0, 38)
-        cast_w(1, "s", 38, 64)
-        quant_w()
-        gather(es[:], es_w[:], cand_t[:])
-        cast_g(0, "s")
-        cast_g(1, "s")
-        cast_g(3, "s")
-        quant_g(0)
-        mm_h(0)
-        quant_g(1)
-        mm_h(1)
-        cast_g(2, "v")
-        quant_g(2)
-        mm_h(2)
-        quant_g(3)
-        mm_h(3)
+        load_scales(xs_w, x_scales)
+        nc.sync.dma_start(out=w_raw[:, 1:, :], in_=w_src[:, 1:, :])
+        load_words(vw, v_words)
+        for u in range(2):
+            load_half(g_raw, g_src, u)
+        load_words(ew, e_words)
+        load_words(xw, x_words)
+        gather(picked[:, :V], es_w[:], cand_t[:])
+        gather(picked[:, V : 2 * V], vs_w[:], cand_t[:])
+        gather(picked[:, 2 * V :], xs_w[:], offs_t[:])
+        lay_planes()
+        vq = tile("vq", [P, V], U32)
         gather(vq[:], vw[:].bitcast(U32), cand_t[:])
-        relu(0)
-        relu(1)
-        relu(2)
-        relu(3)
-        quant_h(0)
-        mm_deep(0, True)
-        quant_h(1)
-        mm_deep(1, True)
-        gather_x(0)
-        mm_wide(0, False)
-        gather_x(1)
-        mm_wide(1, False)
-        quant_h(2)
-        mm_deep(2, True)
-        gather_x(2)
-        mm_wide(2, False)
-        quant_h(3)
-        mm_deep(3, True)
-        gather_x(3)
-        mm_wide(3, False)
-        row_max(0)
-        exp(0)
-        row_max(1)
-        exp(1)
-        row_max(2)
-        exp(2)
+        wq = tile("wq", [P, H], U32)
+        cast_w()
+        quant(wq[:], wsc[:], w_bf[:])
+        for c in (0, 1, 3):
+            cast_g(c, "s", f"g_bf{c}")
+        layer1(0, "gq0")
+        cast_g(2, "v", "w_bf")
+        for c in range(1, NCH):
+            layer1(c, f"gq{c}")
+        for c in range(2):
+            mm(y_ps[c][:], gq[3], gsc[:, cols(3)], wq[:], wsc[:], True, True)
+        eq = shared("eq", [P, V], U32, "w_bf")
+        gather(eq[:], ew[:].bitcast(U32), cand_t[:])
+        for c in range(NCH):
+            relu(c)
+        hq_all = shared("hq_all", [P, S], U32, "ew")
+        xq_all = shared("xq_all", [P, S], U32, "g_bf3")
+        for c in range(NCH):
+            xq[c] = xq_all[:, cols(c)]
+            wide(c, True)
+            if c < 2:
+                deep(c, 1)
+        deep(2, 2)
+        for c in range(NCH - 1):
+            max_exp(c)
         recip(0)
-        row_max(3)
-        exp(3)
-        norm(0, "v")
-        store(0, nc.sync)
-        recip(1)
-        norm(1, "v")
-        store(1, nc.sync)
-        recip(2)
-        norm(2, "v")
-        store(2, nc.sync)
-        recip(3)
-        norm(3, "v")
-        store(3, nc.sync)
+        max_exp(3)
+        for c in range(NCH):
+            if c + 1 < NCH:
+                recip(c + 1)
+            finish(c, "v" if c else "v")

@@ -20,7 +20,11 @@ P = 128
 PACK = 4
 CH = 128
 NCH = S // CH
-HALF = 256
+HALF = 2 * CH
+BLOCK_PARTS = 8
+QUAD = 32
+LIST_COLS = CH // 16
+VECTOR_CHUNK = 2
 
 
 def tile_picked_zwd_soft_p_kernel(tc, x_words, x_scales, e_words, e_scales, v_words, v_scales, gT, w1, offs, cand, out):
@@ -32,22 +36,22 @@ def tile_picked_zwd_soft_p_kernel(tc, x_words, x_scales, e_words, e_scales, v_wo
         def tile(name, shape, dt):
             return sb.tile(shape, dt, name=name, align_bytes=64)
 
-        def shared(name, shape, dt, tag):
-            return sb.tile(shape, dt, name=name, tag=tag, align_bytes=64)
+        def tile_over(earlier, name, shape, dt):
+            return sb.tile(shape, dt, name=name, tag=earlier, align_bytes=64)
 
         cand_t = tile("cand_t", [P, V // 16], U16)
         offs_t = tile("offs_t", [P, S // 16], U16)
-        es_w = shared("es_w", [P, T], U8, "es_w")
-        vs_w = shared("vs_w", [P, T], U8, "vs_w")
-        xs_w = shared("xs_w", [P, T], U8, "xs_w")
+        es_w = tile("es_w", [P, T], U8)
+        vs_w = tile("vs_w", [P, T], U8)
+        xs_w = tile("xs_w", [P, T], U8)
         w_src = w1.rearrange("(p j) c -> p j c", j=PACK)
         g_src = gT.rearrange("(p j) c -> p j c", j=PACK)
         w_raw = tile("w_raw", [P, PACK, H], F32)
-        g_raw = [shared(f"g_raw{u}", [P, PACK, HALF], F32, f"g_raw{u}") for u in range(2)]
+        g_raw = [tile(f"g_raw{u}", [P, PACK, HALF], F32) for u in range(S // HALF)]
         picked = tile("picked", [P, 2 * V + S], U8)
         planes = tile("planes", [P, 2 * V + S], U8)
         es, vs, xs = planes[:, :V], planes[:, V : 2 * V], planes[:, 2 * V :]
-        w_bf = shared("w_bf", [P, H * PACK], BF16, "w_bf")
+        w_bf = tile("w_bf", [P, H * PACK], BF16)
         w_view = w_bf[:].rearrange("p (t m j) -> p m j t", t=PACK, j=PACK)
         wsc = tile("wsc", [P, H], U8)
         gsc = tile("gsc", [P, S], U8)
@@ -55,9 +59,9 @@ def tile_picked_zwd_soft_p_kernel(tc, x_words, x_scales, e_words, e_scales, v_wo
         h_ps = [ps.tile([P, PACK, CH], F32, name=f"h_ps{c}") for c in range(NCH)]
         y_ps = [ps.tile([P, V], F32, name=f"y_ps{c}") for c in range(NCH)]
         h_all = tile("h_all", [P, S * PACK], BF16)
-        g_bf, gq, hq, xq = {}, {}, {}, {}
-        neg_max = [shared(f"neg_max{c}", [P, 1], F32, f"neg_max{c}") for c in range(NCH)]
-        total = [shared(f"total{c}", [P, 1], F32, f"total{c}") for c in range(NCH)]
+        g_bf, gq = {}, {}
+        neg_max = [tile(f"neg_max{c}", [P, 1], F32) for c in range(NCH)]
+        total = [tile(f"total{c}", [P, 1], F32) for c in range(NCH)]
         inv = [tile(f"inv{c}", [P, 1], F32) for c in range(NCH)]
         ex = [tile(f"ex{c}", [P, V], F32) for c in range(NCH)]
         res = [tile(f"res{c}", [P, V], F32) for c in range(NCH)]
@@ -65,24 +69,11 @@ def tile_picked_zwd_soft_p_kernel(tc, x_words, x_scales, e_words, e_scales, v_wo
         def cols(c):
             return slice(CH * c, CH * (c + 1))
 
-        def load_scales(t, src):
-            nc.sync.dma_start(out=t[:].bitcast(I32)[0:P:8, :], in_=src[0].bitcast(I32))
+        def load_scales(dst, src):
+            nc.sync.dma_start(out=dst[:].bitcast(I32)[0:P:BLOCK_PARTS, :], in_=src[0].bitcast(I32))
 
-        def load_words(t, src):
-            nc.sync.dma_start(out=t[:], in_=src[0].rearrange("p n t -> p (n t)").bitcast(I32))
-
-        def load_half(raw, src, u):
-            nc.sync.dma_start(out=raw[u][:], in_=src[:, :, HALF * u : HALF * (u + 1)])
-
-        def lay_planes():
-            for r in range(4):
-                nc.sync.dma_start(out=planes[:].bitcast(I32)[r:P:32, :], in_=picked[:].bitcast(I32)[8 * r : P : 32, :])
-
-        def copy(eng, dst, src):
-            if eng == "v":
-                nc.vector.tensor_copy(dst, src)
-            else:
-                nc.scalar.copy(dst, src)
+        def load_words(dst, src):
+            nc.sync.dma_start(out=dst[:], in_=src[0].rearrange("p n t -> p (n t)").bitcast(I32))
 
         def gather(dst, window, offsets):
             nc.vector.tensor_copy(dst, window.indirect(offsets))
@@ -94,47 +85,39 @@ def tile_picked_zwd_soft_p_kernel(tc, x_words, x_scales, e_words, e_scales, v_wo
             nc.tensor.matmul_mx(out=dst, lhsT=lhs.bitcast(FP8X4), lhsT_scale=lhs_scale,
                                 rhs=rhs.bitcast(FP8X4), rhs_scale=rhs_scale, start=start, stop=stop)
 
-        def cast_w():
-            nc.scalar.copy(w_view, w_raw[:].rearrange("p j (m t) -> p m j t", t=PACK))
-
-        def cast_g(c, eng, tag):
-            g_bf[c] = shared(f"g_bf{c}", [P, CH * PACK], BF16, tag)[:]
+        def round_g(c, copy):
             raw = g_raw[c // 2][:, :, cols(c % 2)]
-            copy(eng, g_bf[c].rearrange("p (n i j) -> p n j i", i=4, j=PACK), raw.rearrange("p j (n i) -> p n j i", i=4))
+            copy(g_bf[c].rearrange("p (n i j) -> p n j i", i=4, j=PACK), raw.rearrange("p j (n i) -> p n j i", i=4))
 
-        def layer1(c, tag):
-            gq[c] = shared(f"gq{c}", [P, CH], U32, tag)[:]
+        def first_layer(c):
+            gq[c] = tile(f"gq{c}", [P, CH], U32)[:]
             quant(gq[c], gsc[:, cols(c)], g_bf[c])
-            for j in range(PACK):
-                mm(h_ps[c][:, j, :], wq[:, cols(j)], wsc[:, cols(j)], gq[c], gsc[:, cols(c)], True, True)
+            for t in range(PACK):
+                mm(h_ps[c][:, t, :], wq[:, cols(t)], wsc[:, cols(t)], gq[c], gsc[:, cols(c)], True, True)
 
         def relu(c):
-            nc.scalar.activation(h_all[:, CH * PACK * c : CH * PACK * (c + 1)].rearrange("p (n j) -> p n j", j=PACK), h_ps[c][:].rearrange("p j n -> p n j"), ACT.Relu)
+            dst = h_all[:, CH * PACK * c : CH * PACK * (c + 1)].rearrange("p (n t) -> p n t", t=PACK)
+            nc.scalar.activation(dst, h_ps[c][:].rearrange("p t n -> p n t"), ACT.Relu)
 
-        def deep(first, n):
-            span = slice(CH * first, CH * (first + n))
-            quant(hq_all[:, span], hsc[:, span], h_all[:, CH * PACK * first : CH * PACK * (first + n)])
-            for c in range(first, first + n):
+        def wide(c):
+            gather(xq_all[:, cols(c)], xw[:].bitcast(U32), offs_t[:, LIST_COLS * c : LIST_COLS * (c + 1)])
+            mm(y_ps[c][:], xq_all[:, cols(c)], xs[:, cols(c)], eq[:], es, True, False)
+
+        def deep(first, count):
+            span = slice(CH * first, CH * (first + count))
+            quant(hq_all[:, span], hsc[:, span], h_all[:, CH * PACK * first : CH * PACK * (first + count)])
+            for c in range(first, first + count):
                 mm(y_ps[c][:], hq_all[:, cols(c)], hsc[:, cols(c)], vq[:], vs, False, True)
-
-        def wide(c, first):
-            gather(xq[c], xw[:].bitcast(U32), offs_t[:, 8 * c : 8 * (c + 1)])
-            mm(y_ps[c][:], xq[c], xs[:, cols(c)], eq[:], es, first, not first)
 
         def max_exp(c):
             nc.vector.tensor_reduce(neg_max[c][:], y_ps[c][:], AX.X, ALU.max, negate=True)
             nc.scalar.activation(ex[c][:], y_ps[c][:], ACT.Exp, bias=neg_max[c][:], accum_out=total[c][:])
 
-        def recip(c):
+        def invert_sum(c):
             nc.vector.reciprocal(inv[c][:], total[c][:])
 
-        def finish(c, eng):
-            if eng == "s":
-                nc.scalar.activation(res[c][:], ex[c][:], ACT.Copy, scale=inv[c][:])
-            elif eng == "g":
-                nc.gpsimd.tensor_scalar(res[c][:], ex[c][:], inv[c][:], 0.0, ALU.mult, ALU.add)
-            else:
-                nc.vector.tensor_scalar(res[c][:], ex[c][:], inv[c][:], None, ALU.mult)
+        def scale_and_store(c):
+            nc.vector.tensor_scalar(res[c][:], ex[c][:], inv[c][:], None, ALU.mult)
             nc.sync.dma_start(out=out[cols(c), :], in_=res[c][:])
 
         warm = tile("warm", [P, 1], F32)
@@ -145,8 +128,9 @@ def tile_picked_zwd_soft_p_kernel(tc, x_words, x_scales, e_words, e_scales, v_wo
         nc.vector.memset(warm[:], 0.0)
         nc.scalar.activation(warm2[:], warm[:], ACT.Exp)
         nc.gpsimd.memset(planes[:].bitcast(I32), 0)
-        vw = shared("vw", [P, T], I32, "vw")
-        ew = shared("ew", [P, T], I32, "ew")
+
+        vw = tile("vw", [P, T], I32)
+        ew = tile("ew", [P, T], I32)
         xw = tile("xw", [P, T], I32)
         nc.sync.dma_start(cand_t[:], cand)
         nc.sync.dma_start(out=w_raw[:, :1, :], in_=w_src[:, :1, :])
@@ -156,44 +140,52 @@ def tile_picked_zwd_soft_p_kernel(tc, x_words, x_scales, e_words, e_scales, v_wo
         load_scales(xs_w, x_scales)
         nc.sync.dma_start(out=w_raw[:, 1:, :], in_=w_src[:, 1:, :])
         load_words(vw, v_words)
-        for u in range(2):
-            load_half(g_raw, g_src, u)
+        for u, raw in enumerate(g_raw):
+            nc.sync.dma_start(out=raw[:], in_=g_src[:, :, HALF * u : HALF * (u + 1)])
         load_words(ew, e_words)
         load_words(xw, x_words)
+
         gather(picked[:, :V], es_w[:], cand_t[:])
         gather(picked[:, V : 2 * V], vs_w[:], cand_t[:])
         gather(picked[:, 2 * V :], xs_w[:], offs_t[:])
-        lay_planes()
+        for r in range(QUAD // BLOCK_PARTS):
+            nc.sync.dma_start(out=planes[:].bitcast(I32)[r:P:QUAD, :], in_=picked[:].bitcast(I32)[BLOCK_PARTS * r : P : QUAD, :])
+
         vq = tile("vq", [P, V], U32)
         gather(vq[:], vw[:].bitcast(U32), cand_t[:])
+
         wq = tile("wq", [P, H], U32)
-        cast_w()
+        nc.scalar.copy(w_view, w_raw[:].rearrange("p j (m t) -> p m j t", t=PACK))
         quant(wq[:], wsc[:], w_bf[:])
-        for c in (0, 1, 3):
-            cast_g(c, "s", f"g_bf{c}")
-        layer1(0, "gq0")
-        cast_g(2, "v", "w_bf")
+
+        for c in range(NCH):
+            if c != VECTOR_CHUNK:
+                g_bf[c] = tile(f"g_bf{c}", [P, CH * PACK], BF16)[:]
+                round_g(c, nc.scalar.copy)
+        first_layer(0)
+        g_bf[VECTOR_CHUNK] = tile_over("w_bf", f"g_bf{VECTOR_CHUNK}", [P, CH * PACK], BF16)[:]
+        round_g(VECTOR_CHUNK, nc.vector.tensor_copy)
         for c in range(1, NCH):
-            layer1(c, f"gq{c}")
-        for c in range(2):
-            mm(y_ps[c][:], gq[3], gsc[:, cols(3)], wq[:], wsc[:], True, True)
-        eq = shared("eq", [P, V], U32, "w_bf")
+            first_layer(c)
+
+        eq = tile_over("w_bf", "eq", [P, V], U32)
         gather(eq[:], ew[:].bitcast(U32), cand_t[:])
         for c in range(NCH):
             relu(c)
-        hq_all = shared("hq_all", [P, S], U32, "ew")
-        xq_all = shared("xq_all", [P, S], U32, "g_bf3")
+
+        hq_all = tile_over("ew", "hq_all", [P, S], U32)
+        xq_all = tile_over(f"g_bf{NCH - 1}", "xq_all", [P, S], U32)
         for c in range(NCH):
-            xq[c] = xq_all[:, cols(c)]
-            wide(c, True)
-            if c < 2:
+            wide(c)
+            if c < NCH // 2:
                 deep(c, 1)
-        deep(2, 2)
+        deep(NCH // 2, NCH // 2)
+
         for c in range(NCH - 1):
             max_exp(c)
-        recip(0)
-        max_exp(3)
+        invert_sum(0)
+        max_exp(NCH - 1)
         for c in range(NCH):
             if c + 1 < NCH:
-                recip(c + 1)
-            finish(c, "v" if c else "v")
+                invert_sum(c + 1)
+            scale_and_store(c)

@@ -70,7 +70,8 @@ def tile_picked_zwd_soft_p_kernel(tc, x_words, x_scales, e_words, e_scales, v_wo
             return slice(CH * c, CH * (c + 1))
 
         def load_scales(dst, src):
-            nc.sync.dma_start(out=dst[:].bitcast(I32)[0:P:BLOCK_PARTS, :], in_=src[0].bitcast(I32))
+            rows = src[0].bitcast(I32)
+            nc.scalar.dma_start(out=dst[:].bitcast(I32)[:QUAD, :], in_=rows.unsqueeze(1).to_broadcast([16, 2, T // 4]))
 
         def load_words(dst, src):
             nc.sync.dma_start(out=dst[:], in_=src[0].rearrange("p n t -> p (n t)").bitcast(I32))
@@ -120,25 +121,24 @@ def tile_picked_zwd_soft_p_kernel(tc, x_words, x_scales, e_words, e_scales, v_wo
             nc.vector.tensor_scalar(res[c][:], ex[c][:], inv[c][:], None, ALU.mult)
             nc.sync.dma_start(out=out[cols(c), :], in_=res[c][:])
 
+        load_scales(es_w, e_scales)
+        load_scales(vs_w, v_scales)
+        load_scales(xs_w, x_scales)
         warm = tile("warm", [P, 1], F32)
         warm2 = tile("warm2", [P, 1], F32)
-        nc.vector.memset(es_w[:].bitcast(I32), 0)
-        nc.gpsimd.memset(vs_w[:].bitcast(I32), 0)
-        nc.vector.memset(xs_w[:].bitcast(I32), 0)
+        for window, engine in ((es_w, nc.vector), (vs_w, nc.gpsimd), (xs_w, nc.gpsimd)):
+            engine.memset(window[:].bitcast(I32)[QUAD : 2 * QUAD, :], 0)
+            engine.memset(window[:].bitcast(I32)[2 * QUAD :, :], 0)
         nc.vector.memset(warm[:], 0.0)
         nc.scalar.activation(warm2[:], warm[:], ACT.Exp)
-        nc.gpsimd.memset(planes[:].bitcast(I32), 0)
+        nc.vector.memset(planes[:].bitcast(I32), 0)
 
         vw = tile("vw", [P, T], I32)
         ew = tile("ew", [P, T], I32)
         xw = tile("xw", [P, T], I32)
         nc.sync.dma_start(cand_t[:], cand)
-        nc.sync.dma_start(out=w_raw[:, :1, :], in_=w_src[:, :1, :])
-        load_scales(es_w, e_scales)
-        load_scales(vs_w, v_scales)
         nc.sync.dma_start(offs_t[:], offs)
-        load_scales(xs_w, x_scales)
-        nc.sync.dma_start(out=w_raw[:, 1:, :], in_=w_src[:, 1:, :])
+        nc.sync.dma_start(out=w_raw[:], in_=w_src)
         load_words(vw, v_words)
         for u, raw in enumerate(g_raw):
             nc.sync.dma_start(out=raw[:], in_=g_src[:, :, HALF * u : HALF * (u + 1)])
@@ -149,10 +149,13 @@ def tile_picked_zwd_soft_p_kernel(tc, x_words, x_scales, e_words, e_scales, v_wo
         gather(picked[:, V : 2 * V], vs_w[:], cand_t[:])
         gather(picked[:, 2 * V :], xs_w[:], offs_t[:])
         for r in range(QUAD // BLOCK_PARTS):
-            nc.sync.dma_start(out=planes[:].bitcast(I32)[r:P:QUAD, :], in_=picked[:].bitcast(I32)[BLOCK_PARTS * r : P : QUAD, :])
+            nc.sync.dma_start(out=planes[:].bitcast(I32)[r:P:QUAD, :], in_=picked[:].bitcast(I32)[2 * r : QUAD : BLOCK_PARTS, :])
 
         vq = tile("vq", [P, V], U32)
         gather(vq[:], vw[:].bitcast(U32), cand_t[:])
+
+        for n in range(2):
+            mm(y_ps[NCH - 1][:], vq[:, :CH], picked[:, V : V + CH], vq[:], picked[:, V : 2 * V], True, True)
 
         wq = tile("wq", [P, H], U32)
         nc.scalar.copy(w_view, w_raw[:].rearrange("p j (m t) -> p m j t", t=PACK))

@@ -154,9 +154,6 @@ def tile_picked_zwd_soft_p_kernel(tc, x_words, x_scales, e_words, e_scales, v_wo
         vq = tile("vq", [P, V], U32)
         gather(vq[:], vw[:].bitcast(U32), cand_t[:])
 
-        for n in range(2):
-            mm(y_ps[NCH - 1][:], vq[:, :CH], picked[:, V : V + CH], vq[:], picked[:, V : 2 * V], True, True)
-
         wq = tile("wq", [P, H], U32)
         nc.scalar.copy(w_view, w_raw[:].rearrange("p j (m t) -> p m j t", t=PACK))
         quant(wq[:], wsc[:], w_bf[:])

@@ -21,8 +21,10 @@ PACK = 4
 CH = 128
 NCH = S // CH
 HALF = 2 * CH
-BLOCK_PARTS = 8
+ROWS = 16
 QUAD = 32
+QUAD_ROWS = 4
+FIRST_ROW = P - ROWS
 LIST_COLS = CH // 16
 VECTOR_CHUNK = 2
 
@@ -70,8 +72,7 @@ def tile_picked_zwd_soft_p_kernel(tc, x_words, x_scales, e_words, e_scales, v_wo
             return slice(CH * c, CH * (c + 1))
 
         def load_scales(dst, src):
-            rows = src[0].bitcast(I32)
-            nc.scalar.dma_start(out=dst[:].bitcast(I32)[:QUAD, :], in_=rows.unsqueeze(1).to_broadcast([16, 2, T // 4]))
+            nc.scalar.dma_start(out=dst[:].bitcast(I32)[FIRST_ROW:, :], in_=src[0].bitcast(I32))
 
         def load_words(dst, src):
             nc.sync.dma_start(out=dst[:], in_=src[0].rearrange("p n t -> p (n t)").bitcast(I32))
@@ -124,13 +125,8 @@ def tile_picked_zwd_soft_p_kernel(tc, x_words, x_scales, e_words, e_scales, v_wo
         load_scales(es_w, e_scales)
         load_scales(vs_w, v_scales)
         load_scales(xs_w, x_scales)
-        warm = tile("warm", [P, 1], F32)
-        warm2 = tile("warm2", [P, 1], F32)
         for window, engine in ((es_w, nc.vector), (vs_w, nc.gpsimd), (xs_w, nc.gpsimd)):
-            engine.memset(window[:].bitcast(I32)[QUAD : 2 * QUAD, :], 0)
-            engine.memset(window[:].bitcast(I32)[2 * QUAD :, :], 0)
-        nc.vector.memset(warm[:], 0.0)
-        nc.scalar.activation(warm2[:], warm[:], ACT.Exp)
+            engine.memset(window[:].bitcast(I32)[:FIRST_ROW, :], 0)
         nc.vector.memset(planes[:].bitcast(I32), 0)
 
         vw = tile("vw", [P, T], I32)
@@ -148,8 +144,9 @@ def tile_picked_zwd_soft_p_kernel(tc, x_words, x_scales, e_words, e_scales, v_wo
         gather(picked[:, :V], es_w[:], cand_t[:])
         gather(picked[:, V : 2 * V], vs_w[:], cand_t[:])
         gather(picked[:, 2 * V :], xs_w[:], offs_t[:])
-        for r in range(QUAD // BLOCK_PARTS):
-            nc.sync.dma_start(out=planes[:].bitcast(I32)[r:P:QUAD, :], in_=picked[:].bitcast(I32)[2 * r : QUAD : BLOCK_PARTS, :])
+        for r in range(QUAD_ROWS):
+            rows = picked[:].bitcast(I32)[FIRST_ROW + r : P : QUAD_ROWS, :]
+            nc.sync.dma_start(out=planes[:].bitcast(I32)[r:P:QUAD, :], in_=rows)
 
         vq = tile("vq", [P, V], U32)
         gather(vq[:], vw[:].bitcast(U32), cand_t[:])

@@ -61,8 +61,8 @@ def tile_picked_zwd_soft_p_kernel(tc, x_words, x_scales, e_words, e_scales, v_wo
         h_ps = [ps.tile([P, PACK, CH], F32, name=f"h_ps{c}") for c in range(NCH)]
         y_ps = [ps.tile([P, V], F32, name=f"y_ps{c}") for c in range(NCH)]
         h_all = tile("h_all", [P, S * PACK], BF16)
-        g_bf, gq = {}, {}
-        neg_max = [tile(f"neg_max{c}", [P, 1], F32) for c in range(NCH)]
+        g_bf, gq, xq, hq = {}, {}, {}, {}
+        neg_max = {}
         total = [tile(f"total{c}", [P, 1], F32) for c in range(NCH)]
         inv = [tile(f"inv{c}", [P, 1], F32) for c in range(NCH)]
         ex = [tile(f"ex{c}", [P, V], F32) for c in range(NCH)]
@@ -101,26 +101,42 @@ def tile_picked_zwd_soft_p_kernel(tc, x_words, x_scales, e_words, e_scales, v_wo
             dst = h_all[:, CH * PACK * c : CH * PACK * (c + 1)].rearrange("p (n t) -> p n t", t=PACK)
             nc.scalar.activation(dst, h_ps[c][:].rearrange("p t n -> p n t"), ACT.Relu)
 
-        def wide(c):
-            gather(xq_all[:, cols(c)], xw[:].bitcast(U32), offs_t[:, LIST_COLS * c : LIST_COLS * (c + 1)])
-            mm(y_ps[c][:], xq_all[:, cols(c)], xs[:, cols(c)], eq[:], es, True, False)
+        def gather_x(first, count, dst):
+            gather(dst, xw[:].bitcast(U32), offs_t[:, LIST_COLS * first : LIST_COLS * (first + count)])
+            for i in range(count):
+                xq[first + i] = dst[:, cols(i)]
 
-        def deep(first, count):
+        def quant_h(first, count, codes):
             span = slice(CH * first, CH * (first + count))
-            quant(hq_all[:, span], hsc[:, span], h_all[:, CH * PACK * first : CH * PACK * (first + count)])
-            for c in range(first, first + count):
-                mm(y_ps[c][:], hq_all[:, cols(c)], hsc[:, cols(c)], vq[:], vs, False, True)
+            quant(codes, hsc[:, span], h_all[:, CH * PACK * first : CH * PACK * (first + count)])
+            for i in range(count):
+                hq[first + i] = codes[:, cols(i)]
 
-        def max_exp(c):
-            nc.vector.tensor_reduce(neg_max[c][:], y_ps[c][:], AX.X, ALU.max, negate=True)
-            nc.scalar.activation(ex[c][:], y_ps[c][:], ACT.Exp, bias=neg_max[c][:], accum_out=total[c][:])
+        def wide(c, opens):
+            mm(y_ps[c][:], xq[c], xs[:, cols(c)], eq[:], es, opens, not opens)
+
+        def deep(c, opens):
+            mm(y_ps[c][:], hq[c], hsc[:, cols(c)], vq[:], vs, opens, not opens)
+
+        def max_exp(c, over=None):
+            if c not in neg_max:
+                neg_max[c] = tile(f"neg_max{c}", [P, 1], F32)[:]
+            nc.vector.tensor_reduce(neg_max[c], y_ps[c][:], AX.X, ALU.max, negate=True)
+            nc.scalar.activation(ex[c][:], y_ps[c][:], ACT.Exp, bias=neg_max[c], accum_out=total[c][:])
 
         def invert_sum(c):
             nc.vector.reciprocal(inv[c][:], total[c][:])
 
-        def scale_and_store(c):
-            nc.vector.tensor_scalar(res[c][:], ex[c][:], inv[c][:], None, ALU.mult)
-            nc.sync.dma_start(out=out[cols(c), :], in_=res[c][:])
+        def store(c, span):
+            nc.sync.dma_start(out=out[cols(c), span], in_=res[c][:, span])
+
+        def scale_on_vector(c, span=slice(0, V)):
+            nc.vector.tensor_scalar(res[c][:, span], ex[c][:, span], inv[c][:], None, ALU.mult)
+            store(c, span)
+
+        def scale_on_scalar(c):
+            nc.scalar.activation(res[c][:], ex[c][:], ACT.Copy, scale=inv[c][:])
+            store(c, slice(0, V))
 
         load_scales(es_w, e_scales)
         load_scales(vs_w, v_scales)
@@ -128,6 +144,11 @@ def tile_picked_zwd_soft_p_kernel(tc, x_words, x_scales, e_words, e_scales, v_wo
         for window, engine in ((es_w, nc.vector), (vs_w, nc.gpsimd), (xs_w, nc.gpsimd)):
             engine.memset(window[:].bitcast(I32)[:FIRST_ROW, :], 0)
         nc.vector.memset(planes[:].bitcast(I32), 0)
+
+        warm_in = tile("warm_in", [P, 1], F32)
+        warm_out = tile("warm_out", [P, 1], F32)
+        nc.vector.memset(warm_in[:], 0.0)
+        nc.scalar.activation(warm_out[:], warm_in[:], ACT.Exp)
 
         vw = tile("vw", [P, T], I32)
         ew = tile("ew", [P, T], I32)
@@ -170,19 +191,30 @@ def tile_picked_zwd_soft_p_kernel(tc, x_words, x_scales, e_words, e_scales, v_wo
         for c in range(NCH):
             relu(c)
 
-        hq_all = tile_over("ew", "hq_all", [P, S], U32)
-        xq_all = tile_over(f"g_bf{NCH - 1}", "xq_all", [P, S], U32)
-        for c in range(NCH):
-            wide(c)
-            if c < NCH // 2:
-                deep(c, 1)
-        deep(NCH // 2, NCH // 2)
+        hq_all = tile_over("g_bf3", "hq_all", [P, S], U32)
+        xq_all = tile_over("gq3", "xq_all", [P, S], U32)
+        quant_h(0, 2, hq_all[:, :HALF])
+        deep(0, True)
+        deep(1, True)
+        gather_x(0, 2, xq_all[:, :HALF])
+        wide(0, False)
+        wide(1, False)
+        gather_x(2, 2, xq_all[:, HALF:])
+        wide(2, True)
+        wide(3, True)
+        quant_h(2, 2, hq_all[:, HALF:])
+        deep(2, False)
+        deep(3, False)
 
         for c in range(NCH - 1):
             max_exp(c)
         invert_sum(0)
         max_exp(NCH - 1)
-        for c in range(NCH):
-            if c + 1 < NCH:
-                invert_sum(c + 1)
-            scale_and_store(c)
+        invert_sum(1)
+        invert_sum(2)
+        scale_on_vector(0, slice(0, V // 2))
+        scale_on_vector(0, slice(V // 2, V))
+        scale_on_vector(1)
+        scale_on_scalar(2)
+        invert_sum(3)
+        scale_on_vector(3)

@@ -20,13 +20,17 @@ P = 128
 PACK = 4
 CH = 128
 NCH = S // CH
-HALF = 2 * CH
+PAIR = 2
+HALF = PAIR * CH
 ROWS = 16
 QUAD = 32
 QUAD_ROWS = 4
 FIRST_ROW = P - ROWS
 LIST_COLS = CH // 16
 VECTOR_CHUNK = 2
+FIRST_PIECE = V // 4
+SHARED_CHUNK = 2
+SHARE = V // 2
 
 
 def tile_picked_zwd_soft_p_kernel(tc, x_words, x_scales, e_words, e_scales, v_words, v_scales, gT, w1, offs, cand, out):
@@ -61,10 +65,12 @@ def tile_picked_zwd_soft_p_kernel(tc, x_words, x_scales, e_words, e_scales, v_wo
         h_ps = [ps.tile([P, PACK, CH], F32, name=f"h_ps{c}") for c in range(NCH)]
         y_ps = [ps.tile([P, V], F32, name=f"y_ps{c}") for c in range(NCH)]
         h_all = tile("h_all", [P, S * PACK], BF16)
-        g_bf, gq, xq, hq = {}, {}, {}, {}
+        g_bf, gq = {}, {}
         neg_max = {}
-        total = [tile(f"total{c}", [P, 1], F32) for c in range(NCH)]
-        inv = [tile(f"inv{c}", [P, 1], F32) for c in range(NCH)]
+        total_all = tile("total_all", [P, NCH], F32)
+        inv_all = tile("inv_all", [P, NCH], F32)
+        total = [total_all[:, c : c + 1] for c in range(NCH)]
+        inv = [inv_all[:, c : c + 1] for c in range(NCH)]
         ex = [tile(f"ex{c}", [P, V], F32) for c in range(NCH)]
         res = [tile(f"res{c}", [P, V], F32) for c in range(NCH)]
 
@@ -88,7 +94,7 @@ def tile_picked_zwd_soft_p_kernel(tc, x_words, x_scales, e_words, e_scales, v_wo
                                 rhs=rhs.bitcast(FP8X4), rhs_scale=rhs_scale, start=start, stop=stop)
 
         def round_g(c, copy):
-            raw = g_raw[c // 2][:, :, cols(c % 2)]
+            raw = g_raw[c // PAIR][:, :, cols(c % PAIR)]
             copy(g_bf[c].rearrange("p (n i j) -> p n j i", i=4, j=PACK), raw.rearrange("p j (n i) -> p n j i", i=4))
 
         def first_layer(c):
@@ -101,42 +107,40 @@ def tile_picked_zwd_soft_p_kernel(tc, x_words, x_scales, e_words, e_scales, v_wo
             dst = h_all[:, CH * PACK * c : CH * PACK * (c + 1)].rearrange("p (n t) -> p n t", t=PACK)
             nc.scalar.activation(dst, h_ps[c][:].rearrange("p t n -> p n t"), ACT.Relu)
 
-        def gather_x(first, count, dst):
-            gather(dst, xw[:].bitcast(U32), offs_t[:, LIST_COLS * first : LIST_COLS * (first + count)])
-            for i in range(count):
-                xq[first + i] = dst[:, cols(i)]
+        def gather_x(pair):
+            entries = offs_t[:, LIST_COLS * PAIR * pair : LIST_COLS * PAIR * (pair + 1)]
+            gather(xq[:, HALF * pair : HALF * (pair + 1)], xw[:].bitcast(U32), entries)
 
-        def quant_h(first, count, codes):
-            span = slice(CH * first, CH * (first + count))
-            quant(codes, hsc[:, span], h_all[:, CH * PACK * first : CH * PACK * (first + count)])
-            for i in range(count):
-                hq[first + i] = codes[:, cols(i)]
+        def quant_h(pair):
+            users = slice(HALF * pair, HALF * (pair + 1))
+            quant(hq[:, users], hsc[:, users], h_all[:, HALF * PACK * pair : HALF * PACK * (pair + 1)])
 
-        def wide(c, opens):
-            mm(y_ps[c][:], xq[c], xs[:, cols(c)], eq[:], es, opens, not opens)
+        def wide(pair, opens):
+            for c in range(PAIR * pair, PAIR * (pair + 1)):
+                mm(y_ps[c][:], xq[:, cols(c)], xs[:, cols(c)], eq[:], es, opens, not opens)
 
-        def deep(c, opens):
-            mm(y_ps[c][:], hq[c], hsc[:, cols(c)], vq[:], vs, opens, not opens)
+        def deep(pair, opens):
+            for c in range(PAIR * pair, PAIR * (pair + 1)):
+                mm(y_ps[c][:], hq[:, cols(c)], hsc[:, cols(c)], vq[:], vs, opens, not opens)
 
-        def max_exp(c, over=None):
-            if c not in neg_max:
-                neg_max[c] = tile(f"neg_max{c}", [P, 1], F32)[:]
+        def max_exp(c):
+            neg_max[c] = tile(f"neg_max{c}", [P, 1], F32)[:]
             nc.vector.tensor_reduce(neg_max[c], y_ps[c][:], AX.X, ALU.max, negate=True)
-            nc.scalar.activation(ex[c][:], y_ps[c][:], ACT.Exp, bias=neg_max[c], accum_out=total[c][:])
+            nc.scalar.activation(ex[c][:], y_ps[c][:], ACT.Exp, bias=neg_max[c], accum_out=total[c])
 
-        def invert_sum(c):
-            nc.vector.reciprocal(inv[c][:], total[c][:])
+        def invert_sums(first, count):
+            nc.vector.reciprocal(inv_all[:, first : first + count], total_all[:, first : first + count])
 
         def store(c, span):
             nc.sync.dma_start(out=out[cols(c), span], in_=res[c][:, span])
 
-        def scale_on_vector(c, span=slice(0, V)):
-            nc.vector.tensor_scalar(res[c][:, span], ex[c][:, span], inv[c][:], None, ALU.mult)
+        def scale_on_vector(c, span):
+            nc.vector.tensor_scalar(res[c][:, span], ex[c][:, span], inv[c], None, ALU.mult)
             store(c, span)
 
-        def scale_on_scalar(c):
-            nc.scalar.activation(res[c][:], ex[c][:], ACT.Copy, scale=inv[c][:])
-            store(c, slice(0, V))
+        def scale_on_scalar(c, span):
+            nc.scalar.activation(res[c][:, span], ex[c][:, span], ACT.Copy, scale=inv[c])
+            store(c, span)
 
         load_scales(es_w, e_scales)
         load_scales(vs_w, v_scales)
@@ -191,30 +195,26 @@ def tile_picked_zwd_soft_p_kernel(tc, x_words, x_scales, e_words, e_scales, v_wo
         for c in range(NCH):
             relu(c)
 
-        hq_all = tile_over("g_bf3", "hq_all", [P, S], U32)
-        xq_all = tile_over("gq3", "xq_all", [P, S], U32)
-        quant_h(0, 2, hq_all[:, :HALF])
-        deep(0, True)
-        deep(1, True)
-        gather_x(0, 2, xq_all[:, :HALF])
-        wide(0, False)
-        wide(1, False)
-        gather_x(2, 2, xq_all[:, HALF:])
-        wide(2, True)
-        wide(3, True)
-        quant_h(2, 2, hq_all[:, HALF:])
-        deep(2, False)
-        deep(3, False)
+        hq = tile_over(f"g_bf{NCH - 1}", "hq", [P, S], U32)
+        xq = tile_over(f"gq{NCH - 1}", "xq", [P, S], U32)
+        quant_h(0)
+        deep(0, opens=True)
+        gather_x(0)
+        wide(0, opens=False)
+        gather_x(1)
+        wide(1, opens=True)
+        quant_h(1)
+        deep(1, opens=False)
 
-        for c in range(NCH - 1):
+        for c in range(NCH):
             max_exp(c)
-        invert_sum(0)
-        max_exp(NCH - 1)
-        invert_sum(1)
-        invert_sum(2)
-        scale_on_vector(0, slice(0, V // 2))
-        scale_on_vector(0, slice(V // 2, V))
-        scale_on_vector(1)
-        scale_on_scalar(2)
-        invert_sum(3)
-        scale_on_vector(3)
+        last = NCH - 1
+        invert_sums(0, PAIR)
+        invert_sums(SHARED_CHUNK, 1)
+        scale_on_vector(0, slice(0, FIRST_PIECE))
+        scale_on_vector(0, slice(FIRST_PIECE, V))
+        scale_on_vector(1, slice(0, V))
+        scale_on_scalar(SHARED_CHUNK, slice(SHARE, V))
+        invert_sums(last, 1)
+        scale_on_vector(SHARED_CHUNK, slice(0, SHARE))
+        scale_on_vector(last, slice(0, V))

@@ -115,13 +115,11 @@ def tile_picked_zwd_soft_p_kernel(tc, x_words, x_scales, e_words, e_scales, v_wo
             users = slice(HALF * pair, HALF * (pair + 1))
             quant(hq[:, users], hsc[:, users], h_all[:, HALF * PACK * pair : HALF * PACK * (pair + 1)])
 
-        def wide(pair, opens):
-            for c in range(PAIR * pair, PAIR * (pair + 1)):
-                mm(y_ps[c][:], xq[:, cols(c)], xs[:, cols(c)], eq[:], es, opens, not opens)
+        def wide(c, opens):
+            mm(y_ps[c][:], xq[:, cols(c)], xs[:, cols(c)], eq[:], es, opens, not opens)
 
-        def deep(pair, opens):
-            for c in range(PAIR * pair, PAIR * (pair + 1)):
-                mm(y_ps[c][:], hq[:, cols(c)], hsc[:, cols(c)], vq[:], vs, opens, not opens)
+        def deep(c, opens):
+            mm(y_ps[c][:], hq[:, cols(c)], hsc[:, cols(c)], vq[:], vs, opens, not opens)
 
         def max_exp(c):
             neg_max[c] = tile(f"neg_max{c}", [P, 1], F32)[:]
@@ -198,13 +196,15 @@ def tile_picked_zwd_soft_p_kernel(tc, x_words, x_scales, e_words, e_scales, v_wo
         hq = tile_over(f"g_bf{NCH - 1}", "hq", [P, S], U32)
         xq = tile_over(f"gq{NCH - 1}", "xq", [P, S], U32)
         quant_h(0)
-        deep(0, opens=True)
         gather_x(0)
-        wide(0, opens=False)
+        for c in range(PAIR):
+            deep(c, opens=True)
+            wide(c, opens=False)
         gather_x(1)
-        wide(1, opens=True)
         quant_h(1)
-        deep(1, opens=False)
+        for c in range(PAIR, NCH):
+            wide(c, opens=True)
+            deep(c, opens=False)
 
         for c in range(NCH):
             max_exp(c)

@@ -52,7 +52,7 @@ def tile_picked_zwd_soft_p_kernel(tc, x_words, x_scales, e_words, e_scales, v_wo
         xs_w = tile("xs_w", [P, T], U8)
         w_src = w1.rearrange("(p j) c -> p j c", j=PACK)
         g_src = gT.rearrange("(p j) c -> p j c", j=PACK)
-        w_raw = tile("w_raw", [P, PACK, H], F32)
+        w_raw = [tile(f"w_raw{u}", [P, PACK, H // 2], F32) for u in range(2)]
         g_raw = [tile(f"g_raw{u}", [P, PACK, HALF], F32) for u in range(S // HALF)]
         picked = tile("picked", [P, 2 * V + S], U8)
         planes = tile("planes", [P, 2 * V + S], U8)
@@ -98,8 +98,6 @@ def tile_picked_zwd_soft_p_kernel(tc, x_words, x_scales, e_words, e_scales, v_wo
             copy(g_bf[c].rearrange("p (n i j) -> p n j i", i=4, j=PACK), raw.rearrange("p j (n i) -> p n j i", i=4))
 
         def first_layer(c):
-            gq[c] = tile(f"gq{c}", [P, CH], U32)[:]
-            quant(gq[c], gsc[:, cols(c)], g_bf[c])
             for t in range(PACK):
                 mm(h_ps[c][:, t, :], wq[:, cols(t)], wsc[:, cols(t)], gq[c], gsc[:, cols(c)], True, True)
 
@@ -157,7 +155,8 @@ def tile_picked_zwd_soft_p_kernel(tc, x_words, x_scales, e_words, e_scales, v_wo
         xw = tile("xw", [P, T], I32)
         nc.sync.dma_start(cand_t[:], cand)
         nc.sync.dma_start(offs_t[:], offs)
-        nc.sync.dma_start(out=w_raw[:], in_=w_src)
+        for u, raw in enumerate(w_raw):
+            nc.sync.dma_start(out=raw[:], in_=w_src[:, :, H // 2 * u : H // 2 * (u + 1)])
         load_words(vw, v_words)
         for u, raw in enumerate(g_raw):
             nc.sync.dma_start(out=raw[:], in_=g_src[:, :, HALF * u : HALF * (u + 1)])
@@ -175,26 +174,36 @@ def tile_picked_zwd_soft_p_kernel(tc, x_words, x_scales, e_words, e_scales, v_wo
         gather(vq[:], vw[:].bitcast(U32), cand_t[:])
 
         wq = tile("wq", [P, H], U32)
-        nc.scalar.copy(w_view, w_raw[:].rearrange("p j (m t) -> p m j t", t=PACK))
+        for u, raw in enumerate(w_raw):
+            nc.scalar.copy(w_view[:, P // 2 * u : P // 2 * (u + 1)], raw[:].rearrange("p j (m t) -> p m j t", t=PACK))
         quant(wq[:], wsc[:], w_bf[:])
 
+        late_bf = tile("late_bf", [P, HALF * PACK], BF16)
+        late_q = tile("late_q", [P, HALF], U32)
+        for c in range(PAIR):
+            g_bf[c] = tile(f"g_bf{c}", [P, CH * PACK], BF16)[:]
+            gq[c] = tile(f"gq{c}", [P, CH], U32)[:]
+            g_bf[PAIR + c] = late_bf[:, CH * PACK * c : CH * PACK * (c + 1)]
+            gq[PAIR + c] = late_q[:, cols(c)]
         for c in range(NCH):
             if c != VECTOR_CHUNK:
-                g_bf[c] = tile(f"g_bf{c}", [P, CH * PACK], BF16)[:]
                 round_g(c, nc.scalar.copy)
+        quant(gq[0], gsc[:, cols(0)], g_bf[0])
         first_layer(0)
-        g_bf[VECTOR_CHUNK] = tile_over("w_bf", f"g_bf{VECTOR_CHUNK}", [P, CH * PACK], BF16)[:]
         round_g(VECTOR_CHUNK, nc.vector.tensor_copy)
-        for c in range(1, NCH):
+        quant(gq[1], gsc[:, cols(1)], g_bf[1])
+        first_layer(1)
+        quant(late_q[:], gsc[:, HALF:], late_bf[:])
+        for c in range(PAIR, NCH):
             first_layer(c)
 
-        eq = tile_over("w_bf", "eq", [P, V], U32)
+        eq = tile_over("g_bf1", "eq", [P, V], U32)
         gather(eq[:], ew[:].bitcast(U32), cand_t[:])
         for c in range(NCH):
             relu(c)
 
-        hq = tile_over(f"g_bf{NCH - 1}", "hq", [P, S], U32)
-        xq = tile_over(f"gq{NCH - 1}", "xq", [P, S], U32)
+        hq = tile_over("late_bf", "hq", [P, S], U32)
+        xq = tile_over("late_q", "xq", [P, S], U32)
         quant_h(0)
         gather_x(0)
         for c in range(PAIR):

@@ -28,7 +28,7 @@ QUAD_ROWS = 4
 FIRST_ROW = P - ROWS
 LIST_COLS = CH // 16
 VECTOR_CHUNK = 2
-FIRST_PIECE = V // 4
+FIRST_PIECE = 3 * V // 8
 SHARED_CHUNK = 2
 SHARE = V // 2
 
@@ -154,9 +154,9 @@ def tile_picked_zwd_soft_p_kernel(tc, x_words, x_scales, e_words, e_scales, v_wo
         ew = tile("ew", [P, T], I32)
         xw = tile("xw", [P, T], I32)
         nc.sync.dma_start(cand_t[:], cand)
+        nc.sync.dma_start(out=w_raw[0][:], in_=w_src[:, :, : H // 2])
         nc.sync.dma_start(offs_t[:], offs)
-        for u, raw in enumerate(w_raw):
-            nc.sync.dma_start(out=raw[:], in_=w_src[:, :, H // 2 * u : H // 2 * (u + 1)])
+        nc.sync.dma_start(out=w_raw[1][:], in_=w_src[:, :, H // 2 :])
         load_words(vw, v_words)
         for u, raw in enumerate(g_raw):
             nc.sync.dma_start(out=raw[:], in_=g_src[:, :, HALF * u : HALF * (u + 1)])

@@ -28,7 +28,7 @@ QUAD_ROWS = 4
 FIRST_ROW = P - ROWS
 LIST_COLS = CH // 16
 VECTOR_CHUNK = 2
-FIRST_PIECE = 3 * V // 8
+FIRST_PIECE = V // 2
 SHARED_CHUNK = 2
 SHARE = V // 2
 
@@ -215,13 +215,15 @@ def tile_picked_zwd_soft_p_kernel(tc, x_words, x_scales, e_words, e_scales, v_wo
             wide(c, opens=True)
             deep(c, opens=False)
 
-        for c in range(NCH):
-            max_exp(c)
         last = NCH - 1
-        invert_sums(0, PAIR)
-        invert_sums(SHARED_CHUNK, 1)
+        for c in range(last):
+            max_exp(c)
+        invert_sums(0, 1)
+        max_exp(last)
         scale_on_vector(0, slice(0, FIRST_PIECE))
+        invert_sums(1, 1)
         scale_on_vector(0, slice(FIRST_PIECE, V))
+        invert_sums(SHARED_CHUNK, 1)
         scale_on_vector(1, slice(0, V))
         scale_on_scalar(SHARED_CHUNK, slice(SHARE, V))
         invert_sums(last, 1)

@@ -132,11 +132,9 @@ def tile_picked_zwd_soft_p_kernel(tc, x_words, x_scales, e_words, e_scales, v_wo
 
         def scale_on_vector(c, span):
             nc.vector.tensor_scalar(res[c][:, span], ex[c][:, span], inv[c], None, ALU.mult)
-            store(c, span)
 
         def scale_on_scalar(c, span):
             nc.scalar.activation(res[c][:, span], ex[c][:, span], ACT.Copy, scale=inv[c])
-            store(c, span)
 
         load_scales(es_w, e_scales)
         load_scales(vs_w, v_scales)
@@ -220,12 +218,18 @@ def tile_picked_zwd_soft_p_kernel(tc, x_words, x_scales, e_words, e_scales, v_wo
             max_exp(c)
         invert_sums(0, 1)
         max_exp(last)
+        whole = slice(0, V)
         scale_on_vector(0, slice(0, FIRST_PIECE))
+        store(0, slice(0, FIRST_PIECE))
         invert_sums(1, 1)
         scale_on_vector(0, slice(FIRST_PIECE, V))
+        store(0, slice(FIRST_PIECE, V))
         invert_sums(SHARED_CHUNK, 1)
-        scale_on_vector(1, slice(0, V))
+        scale_on_vector(1, whole)
+        store(1, whole)
         scale_on_scalar(SHARED_CHUNK, slice(SHARE, V))
         invert_sums(last, 1)
         scale_on_vector(SHARED_CHUNK, slice(0, SHARE))
-        scale_on_vector(last, slice(0, V))
+        store(SHARED_CHUNK, whole)
+        scale_on_vector(last, whole)
+        store(last, whole)

from contextlib import ExitStack

import concourse.mybir as mybir

K, T, S, V, H = 512, 1024, 512, 512, 512
FLOPS = 2 * K * H * S + 2 * K * S * V + 2 * H * S * V

F32 = mybir.dt.float32
BF16 = mybir.dt.bfloat16
I32 = mybir.dt.int32
U32 = mybir.dt.uint32
U16 = mybir.dt.uint16
U8 = mybir.dt.uint8
FP8X4 = mybir.dt.float8_e4m3fn_x4
ACT = mybir.ActivationFunctionType
ALU = mybir.AluOpType
AX = mybir.AxisListType

P = 128
PACK = 4
CH = 128
NCH = S // CH
PAIR = 2
HALF = PAIR * CH
ROWS = 16
QUAD = 32
QUAD_ROWS = 4
FIRST_ROW = P - ROWS
LIST_COLS = CH // 16
VECTOR_CHUNK = 2
FIRST_PIECE = V // 2
SHARED_CHUNK = 2
SHARE = V // 2


def tile_picked_zwd_soft_p_kernel(tc, x_words, x_scales, e_words, e_scales, v_words, v_scales, gT, w1, offs, cand, out):
    nc = tc.nc
    with ExitStack() as ctx:
        sb = ctx.enter_context(tc.tile_pool(name="sb", bufs=1))
        ps = ctx.enter_context(tc.psum_pool(name="ps", bufs=1))

        def tile(name, shape, dt):
            return sb.tile(shape, dt, name=name, align_bytes=64)

        def tile_over(earlier, name, shape, dt):
            return sb.tile(shape, dt, name=name, tag=earlier, align_bytes=64)

        cand_t = tile("cand_t", [P, V // 16], U16)
        offs_t = tile("offs_t", [P, S // 16], U16)
        es_w = tile("es_w", [P, T], U8)
        vs_w = tile("vs_w", [P, T], U8)
        xs_w = tile("xs_w", [P, T], U8)
        w_src = w1.rearrange("(p j) c -> p j c", j=PACK)
        g_src = gT.rearrange("(p j) c -> p j c", j=PACK)
        w_raw = [tile(f"w_raw{u}", [P, PACK, H // 2], F32) for u in range(2)]
        g_raw = [tile(f"g_raw{u}", [P, PACK, HALF], F32) for u in range(S // HALF)]
        picked = tile("picked", [P, 2 * V + S], U8)
        planes = tile("planes", [P, 2 * V + S], U8)
        es, vs, xs = planes[:, :V], planes[:, V : 2 * V], planes[:, 2 * V :]
        w_bf = tile("w_bf", [P, H * PACK], BF16)
        w_view = w_bf[:].rearrange("p (t m j) -> p m j t", t=PACK, j=PACK)
        wsc = tile("wsc", [P, H], U8)
        gsc = tile("gsc", [P, S], U8)
        hsc = tile("hsc", [P, S], U8)
        h_ps = [ps.tile([P, PACK, CH], F32, name=f"h_ps{c}") for c in range(NCH)]
        y_ps = [ps.tile([P, V], F32, name=f"y_ps{c}") for c in range(NCH)]
        h_all = tile("h_all", [P, S * PACK], BF16)
        g_bf, gq = {}, {}
        neg_max = {}
        total_all = tile("total_all", [P, NCH], F32)
        inv_all = tile("inv_all", [P, NCH], F32)
        total = [total_all[:, c : c + 1] for c in range(NCH)]
        inv = [inv_all[:, c : c + 1] for c in range(NCH)]
        ex = [tile(f"ex{c}", [P, V], F32) for c in range(NCH)]
        res = [tile(f"res{c}", [P, V], F32) for c in range(NCH)]

        def cols(c):
            return slice(CH * c, CH * (c + 1))

        def load_scales(dst, src):
            nc.scalar.dma_start(out=dst[:].bitcast(I32)[FIRST_ROW:, :], in_=src[0].bitcast(I32))

        def load_words(dst, src):
            nc.sync.dma_start(out=dst[:], in_=src[0].rearrange("p n t -> p (n t)").bitcast(I32))

        def gather(dst, window, offsets):
            nc.vector.tensor_copy(dst, window.indirect(offsets))

        def quant(codes, scales, src):
            nc.vector.quantize_mx(out=codes.bitcast(FP8X4), scales=scales, in_=src)

        def mm(dst, lhs, lhs_scale, rhs, rhs_scale, start, stop):
            nc.tensor.matmul_mx(out=dst, lhsT=lhs.bitcast(FP8X4), lhsT_scale=lhs_scale,
                                rhs=rhs.bitcast(FP8X4), rhs_scale=rhs_scale, start=start, stop=stop)

        def round_g(c, copy):
            raw = g_raw[c // PAIR][:, :, cols(c % PAIR)]
            copy(g_bf[c].rearrange("p (n i j) -> p n j i", i=4, j=PACK), raw.rearrange("p j (n i) -> p n j i", i=4))

        def first_layer(c):
            for t in range(PACK):
                mm(h_ps[c][:, t, :], wq[:, cols(t)], wsc[:, cols(t)], gq[c], gsc[:, cols(c)], True, True)

        def relu(c):
            dst = h_all[:, CH * PACK * c : CH * PACK * (c + 1)].rearrange("p (n t) -> p n t", t=PACK)
            nc.scalar.activation(dst, h_ps[c][:].rearrange("p t n -> p n t"), ACT.Relu)

        def gather_x(pair):
            entries = offs_t[:, LIST_COLS * PAIR * pair : LIST_COLS * PAIR * (pair + 1)]
            gather(xq[:, HALF * pair : HALF * (pair + 1)], xw[:].bitcast(U32), entries)

        def quant_h(pair):
            users = slice(HALF * pair, HALF * (pair + 1))
            quant(hq[:, users], hsc[:, users], h_all[:, HALF * PACK * pair : HALF * PACK * (pair + 1)])

        def wide(c, opens):
            mm(y_ps[c][:], xq[:, cols(c)], xs[:, cols(c)], eq[:], es, opens, not opens)

        def deep(c, opens):
            mm(y_ps[c][:], hq[:, cols(c)], hsc[:, cols(c)], vq[:], vs, opens, not opens)

        def max_exp(c):
            neg_max[c] = tile(f"neg_max{c}", [P, 1], F32)[:]
            nc.vector.tensor_reduce(neg_max[c], y_ps[c][:], AX.X, ALU.max, negate=True)
            nc.scalar.activation(ex[c][:], y_ps[c][:], ACT.Exp, bias=neg_max[c], accum_out=total[c])

        def invert_sums(first, count):
            nc.vector.reciprocal(inv_all[:, first : first + count], total_all[:, first : first + count])

        def store(c, span):
            nc.sync.dma_start(out=out[cols(c), span], in_=res[c][:, span])

        def scale_on_vector(c, span):
            nc.vector.tensor_scalar(res[c][:, span], ex[c][:, span], inv[c], None, ALU.mult)

        def scale_on_scalar(c, span):
            nc.scalar.activation(res[c][:, span], ex[c][:, span], ACT.Copy, scale=inv[c])

        load_scales(es_w, e_scales)
        load_scales(vs_w, v_scales)
        load_scales(xs_w, x_scales)
        for window, engine in ((es_w, nc.vector), (vs_w, nc.gpsimd), (xs_w, nc.gpsimd)):
            engine.memset(window[:].bitcast(I32)[:FIRST_ROW, :], 0)
        nc.vector.memset(planes[:].bitcast(I32), 0)

        warm_in = tile("warm_in", [P, 1], F32)
        warm_out = tile("warm_out", [P, 1], F32)
        nc.vector.memset(warm_in[:], 0.0)
        nc.scalar.activation(warm_out[:], warm_in[:], ACT.Exp)

        vw = tile("vw", [P, T], I32)
        ew = tile("ew", [P, T], I32)
        xw = tile("xw", [P, T], I32)
        nc.sync.dma_start(cand_t[:], cand)
        nc.sync.dma_start(out=w_raw[0][:], in_=w_src[:, :, : H // 2])
        nc.sync.dma_start(offs_t[:], offs)
        nc.sync.dma_start(out=w_raw[1][:], in_=w_src[:, :, H // 2 :])
        load_words(vw, v_words)
        for u, raw in enumerate(g_raw):
            nc.sync.dma_start(out=raw[:], in_=g_src[:, :, HALF * u : HALF * (u + 1)])
        load_words(ew, e_words)
        load_words(xw, x_words)

        gather(picked[:, :V], es_w[:], cand_t[:])
        gather(picked[:, V : 2 * V], vs_w[:], cand_t[:])
        gather(picked[:, 2 * V :], xs_w[:], offs_t[:])
        for r in range(QUAD_ROWS):
            rows = picked[:].bitcast(I32)[FIRST_ROW + r : P : QUAD_ROWS, :]
            nc.sync.dma_start(out=planes[:].bitcast(I32)[r:P:QUAD, :], in_=rows)

        vq = tile("vq", [P, V], U32)
        gather(vq[:], vw[:].bitcast(U32), cand_t[:])

        wq = tile("wq", [P, H], U32)
        for u, raw in enumerate(w_raw):
            nc.scalar.copy(w_view[:, P // 2 * u : P // 2 * (u + 1)], raw[:].rearrange("p j (m t) -> p m j t", t=PACK))
        quant(wq[:], wsc[:], w_bf[:])

        late_bf = tile("late_bf", [P, HALF * PACK], BF16)
        late_q = tile("late_q", [P, HALF], U32)
        for c in range(PAIR):
            g_bf[c] = tile(f"g_bf{c}", [P, CH * PACK], BF16)[:]
            gq[c] = tile(f"gq{c}", [P, CH], U32)[:]
            g_bf[PAIR + c] = late_bf[:, CH * PACK * c : CH * PACK * (c + 1)]
            gq[PAIR + c] = late_q[:, cols(c)]
        for c in range(NCH):
            if c != VECTOR_CHUNK:
                round_g(c, nc.scalar.copy)
        quant(gq[0], gsc[:, cols(0)], g_bf[0])
        first_layer(0)
        round_g(VECTOR_CHUNK, nc.vector.tensor_copy)
        quant(gq[1], gsc[:, cols(1)], g_bf[1])
        first_layer(1)
        quant(late_q[:], gsc[:, HALF:], late_bf[:])
        for c in range(PAIR, NCH):
            first_layer(c)

        eq = tile_over("g_bf1", "eq", [P, V], U32)
        gather(eq[:], ew[:].bitcast(U32), cand_t[:])
        for c in range(NCH):
            relu(c)

        hq = tile_over("late_bf", "hq", [P, S], U32)
        xq = tile_over("late_q", "xq", [P, S], U32)
        quant_h(0)
        gather_x(0)
        for c in range(PAIR):
            deep(c, opens=True)
            wide(c, opens=False)
        gather_x(1)
        quant_h(1)
        for c in range(PAIR, NCH):
            wide(c, opens=True)
            deep(c, opens=False)

        last = NCH - 1
        for c in range(last):
            max_exp(c)
        invert_sums(0, 1)
        max_exp(last)
        whole = slice(0, V)
        scale_on_vector(0, slice(0, FIRST_PIECE))
        store(0, slice(0, FIRST_PIECE))
        invert_sums(1, 1)
        scale_on_vector(0, slice(FIRST_PIECE, V))
        store(0, slice(FIRST_PIECE, V))
        invert_sums(SHARED_CHUNK, 1)
        scale_on_vector(1, whole)
        store(1, whole)
        scale_on_scalar(SHARED_CHUNK, slice(SHARE, V))
        invert_sums(last, 1)
        scale_on_vector(SHARED_CHUNK, slice(0, SHARE))
        store(SHARED_CHUNK, whole)
        scale_on_vector(last, whole)
        store(last, whole)
